import numpy as np
import ml_dtypes


def mxq(x, axis, fmt="e4m3"):
    dtype, down = {"e4m3": (ml_dtypes.float8_e4m3fn, 7), "e5m2": (ml_dtypes.float8_e5m2, 14)}[fmt]
    v = np.moveaxis(np.asarray(x, np.float32).astype(ml_dtypes.bfloat16).astype(np.float64), axis, -1)
    blocks = v.reshape(v.shape[:-1] + (-1, 32))
    amax = np.abs(blocks).max(-1, keepdims=True)
    byte = np.maximum(np.where(amax > 0, np.frexp(amax)[1] - 1 + 127, 0) - down, 1)
    scale = np.exp2(byte - 127.0)
    codes = (blocks / scale).astype(np.float32).astype(dtype).astype(np.float64)
    return np.moveaxis((codes * scale).reshape(v.shape), -1, axis)


WIDE = False


def mx_kscale(k):
    if not WIDE:
        return np.ones(k)
    levels = np.array([10, -10, 5, -5, 0])
    if k % 512:
        return np.exp2(np.random.permutation(np.resize(levels, k // 32))).repeat(32)
    a = np.empty((k // 512, 16))
    for p in range(k // 512):
        a[p, :8] = np.random.permutation(np.resize(levels, 8))
        for g in range(8):
            far = levels[np.abs(levels - a[p, g]) >= 10]
            a[p, g + 8] = far[np.random.randint(len(far))]
    return np.exp2(a.ravel()).repeat(32)


def f64(x):
    return np.asarray(x).astype(np.float64)


def striped(idx):
    return np.tile(idx.reshape(-1, 16).T, (8, 1)).astype(np.uint16)


def unstriped(offs):
    return offs[:16].T.reshape(-1).astype(np.int64)


K, T, E, C, N = 2048, 512, 2, 256, 128


def by_expert(wq, xq):
    return np.concatenate([wq[e].T @ xq[:, e * C:(e + 1) * C] for e in range(E)], axis=1)


def setup_inputs():
    n = np.random.standard_normal
    s = mx_kscale(K)[:, None]
    return {
        "xT": (n((K, T)) * s).astype(np.float32),
        "w": (n((E, K, N)) / np.sqrt(K) / s[None]).astype(np.float32),
        "b": (0.3 * n((N, E))).astype(np.float32),
        "gate": np.tile(np.random.uniform(0.2, 1.0, E * C), (N, 1)).astype(np.float32),
        "offs": striped(np.random.permutation(T)[:E * C]),
    }


def reference(xT, w, b, gate, offs):
    idx = unstriped(offs)
    xq = mxq(f64(xT)[:, idx], 0, "e4m3")
    y = by_expert(mxq(f64(w), 1, "e4m3"), xq)
    y = y + np.repeat(f64(b), C, axis=1)
    out = np.zeros((N, T))
    out[:, idx] = f64(gate) * y
    return out

@@ -1,0 +1,142 @@
+from contextlib import ExitStack
+
+import concourse.mybir as mybir
+
+K, T, E, C, N = 2048, 512, 2, 256, 128
+FLOPS = 2 * K * N * E * C
+
+F32 = mybir.dt.float32
+BF16 = mybir.dt.bfloat16
+U32 = mybir.dt.uint32
+U16 = mybir.dt.uint16
+U8 = mybir.dt.uint8
+FP8X4 = mybir.dt.float8_e4m3fn_x4
+IDENT = mybir.ActivationFunctionType.Identity
+MULT = mybir.AluOpType.mult
+
+P = 128
+PACK = 4
+PASSES = K // (P * PACK)
+LCOLS = C // 16
+
+
+def tile_routed_moe_kernel(tc, xT, w, b, gate, offs, out):
+    nc = tc.nc
+    with ExitStack() as ctx:
+        lists = ctx.enter_context(tc.tile_pool(name="lists", bufs=1))
+        keep = ctx.enter_context(tc.tile_pool(name="keep", bufs=1))
+        ring = ctx.enter_context(tc.tile_pool(name="ring", bufs=3))
+        psum = ctx.enter_context(tc.psum_pool(name="psum", bufs=1))
+
+        offsets = lists.tile([P, E * C // 16], U16, name="offsets")
+        nc.sync.dma_start(offsets[:], offs)
+
+        warm_in = keep.tile([P, 1], F32, name="warm_in")
+        warm_out = keep.tile([P, 1], F32, name="warm_out")
+        nc.gpsimd.memset(warm_in[:], 0.0)
+        nc.scalar.activation(warm_out[:], warm_in[:], IDENT)
+
+        x_view = xT.rearrange("(g p t) n -> g p t n", p=P, t=PACK)
+        w_view = w.rearrange("e (g p j) n -> g p e j n", p=P, j=PACK)
+        planes = []
+        w_raw = []
+        for g in range(PASSES):
+            row = []
+            for t in range(PACK):
+                plane = keep.tile([P, T], F32, name="plane%d_%d" % (g, t))
+                nc.sync.dma_start(plane[:], x_view[g, :, t, :])
+                row.append(plane)
+            planes.append(row)
+            raw = keep.tile([P, E, PACK, N], F32, name="w_raw%d" % g)
+            nc.sync.dma_start(raw[:], w_view[g])
+            w_raw.append(raw)
+        b_sb = keep.tile([P, E], F32, name="b_sb")
+        nc.sync.dma_start(b_sb[:], b)
+        gate_sb = keep.tile([P, E * C], F32, name="gate_sb")
+        nc.sync.dma_start(gate_sb[:], gate)
+
+        acc = [psum.tile([P, C], F32, name="acc%d" % e) for e in range(E)]
+        result = keep.tile([P, T], F32, name="result")
+
+        w_codes = {}
+        w_scales = {}
+        x_grouped = {}
+
+        def weights_interleave(g):
+            grouped = ring.tile([P, E, N, PACK], BF16, name="w_grouped", align_bytes=64)
+            nc.scalar.copy(out=grouped[:], in_=w_raw[g][:].rearrange("p e j n -> p e n j"))
+            return grouped
+
+        def weights_quantize(g, grouped):
+            codes = keep.tile([P, E * N], U32, name="w_codes%d" % g, align_bytes=64)
+            scales = keep.tile([P, E * N], U8, name="w_scales%d" % g, align_bytes=64)
+            nc.vector.quantize_mx(
+                out=codes[:].bitcast(FP8X4),
+                scales=scales[:],
+                in_=grouped[:].rearrange("p e n j -> p (e n j)"),
+            )
+            w_codes[g] = codes
+            w_scales[g] = scales
+
+        def gather(g, e):
+            picked = ring.tile([P, PACK, C], F32, name="picked")
+            for t in range(PACK):
+                nc.vector.tensor_copy(
+                    picked[:, t, :],
+                    planes[g][t][:].indirect(offsets[:, e * LCOLS : (e + 1) * LCOLS]),
+                )
+            grouped = ring.tile([P, C, PACK], BF16, name="x_grouped", align_bytes=64)
+            nc.scalar.copy(out=grouped[:], in_=picked[:].rearrange("p t n -> p n t"))
+            x_grouped[(g, e)] = grouped
+
+        def multiply(g, e):
+            codes = ring.tile([P, C], U32, name="x_codes", align_bytes=64)
+            scales = ring.tile([P, C], U8, name="x_scales", align_bytes=64)
+            nc.vector.quantize_mx(
+                out=codes[:].bitcast(FP8X4),
+                scales=scales[:],
+                in_=x_grouped[(g, e)][:].rearrange("p n t -> p (n t)"),
+            )
+            nc.tensor.matmul_mx(
+                out=acc[e][:],
+                lhsT=w_codes[g][:, e * N : (e + 1) * N].bitcast(FP8X4),
+                lhsT_scale=w_scales[g][:, e * N : (e + 1) * N],
+                rhs=codes[:].bitcast(FP8X4),
+                rhs_scale=scales[:],
+                start=(g == 0),
+                stop=(g == PASSES - 1),
+            )
+
+        biased = {}
+
+        def add_bias(e):
+            y = keep.tile([P, C], F32, name="y%d" % e)
+            nc.scalar.activation(y[:], acc[e][:], IDENT, bias=b_sb[:, e : e + 1])
+            biased[e] = y
+
+        def scatter(e):
+            nc.vector.tensor_tensor(
+                result[:].indirect(offsets[:, e * LCOLS : (e + 1) * LCOLS]),
+                biased[e][:],
+                gate_sb[:, e * C : (e + 1) * C],
+                MULT,
+            )
+
+        steps = [(0, 0), (0, 1), (1, 0), (1, 1), (2, 0), (3, 0), (2, 1), (3, 1)]
+        before = None
+        for g, e in steps:
+            w_grouped = weights_interleave(g) if e == 0 else None
+            gather(g, e)
+            if w_grouped is not None:
+                weights_quantize(g, w_grouped)
+            if before is not None:
+                multiply(before[0], before[1])
+                if before == (3, 0):
+                    add_bias(0)
+                if before == (2, 1):
+                    scatter(0)
+            before = (g, e)
+        multiply(before[0], before[1])
+        add_bias(1)
+        scatter(1)
+        nc.sync.dma_start(out, result[:])

@@ -12,12 +12,17 @@ U16 = mybir.dt.uint16
 U8 = mybir.dt.uint8
 FP8X4 = mybir.dt.float8_e4m3fn_x4
 IDENT = mybir.ActivationFunctionType.Identity
+COPY = mybir.ActivationFunctionType.Copy
 MULT = mybir.AluOpType.mult
 
 P = 128
 PACK = 4
 PASSES = K // (P * PACK)
-LCOLS = C // 16
+
+LOADS = [["x",0,4],["x",3,2],["x",1,2],["w",0,1],["w",1,1],["x",2,2],["w",2,1],["w",3,1]]
+SCALAR_PASSES = [3]
+VECTOR_PASSES = [0,1,2]
+GROUPS = [(0, 256), (256, 384), (384, 512)]
 
 
 def tile_routed_moe_kernel(tc, xT, w, b, gate, offs, out):
@@ -25,7 +30,6 @@ def tile_routed_moe_kernel(tc, xT, w, b, gate, offs, out):
     with ExitStack() as ctx:
         lists = ctx.enter_context(tc.tile_pool(name="lists", bufs=1))
         keep = ctx.enter_context(tc.tile_pool(name="keep", bufs=1))
-        ring = ctx.enter_context(tc.tile_pool(name="ring", bufs=3))
         psum = ctx.enter_context(tc.psum_pool(name="psum", bufs=1))
 
         offsets = lists.tile([P, E * C // 16], U16, name="offsets")
@@ -38,105 +42,139 @@ def tile_routed_moe_kernel(tc, xT, w, b, gate, offs, out):
 
         x_view = xT.rearrange("(g p t) n -> g p t n", p=P, t=PACK)
         w_view = w.rearrange("e (g p j) n -> g p e j n", p=P, j=PACK)
-        planes = []
-        w_raw = []
-        for g in range(PASSES):
-            row = []
-            for t in range(PACK):
-                plane = keep.tile([P, T], F32, name="plane%d_%d" % (g, t))
-                nc.sync.dma_start(plane[:], x_view[g, :, t, :])
-                row.append(plane)
-            planes.append(row)
-            raw = keep.tile([P, E, PACK, N], F32, name="w_raw%d" % g)
-            nc.sync.dma_start(raw[:], w_view[g])
-            w_raw.append(raw)
+        x_raw = {}
+        w_raw = {}
+        for kind, g, pieces in LOADS:
+            if kind == "x":
+                raw = keep.tile([P, PACK, T], F32, name="x_raw%d" % g)
+                step = PACK // pieces
+                for t0 in range(0, PACK, step):
+                    nc.sync.dma_start(raw[:, t0 : t0 + step, :], x_view[g, :, t0 : t0 + step, :])
+                x_raw[g] = raw
+            else:
+                raw = keep.tile([P, E, PACK, N], F32, name="w_raw%d" % g)
+                nc.sync.dma_start(raw[:], w_view[g])
+                w_raw[g] = raw
         b_sb = keep.tile([P, E], F32, name="b_sb")
         nc.sync.dma_start(b_sb[:], b)
         gate_sb = keep.tile([P, E * C], F32, name="gate_sb")
         nc.sync.dma_start(gate_sb[:], gate)
 
-        acc = [psum.tile([P, C], F32, name="acc%d" % e) for e in range(E)]
+        acc = [psum.tile([P, s1 - s0], F32, name="acc%d" % i) for i, (s0, s1) in enumerate(GROUPS)]
         result = keep.tile([P, T], F32, name="result")
 
+        x_grouped = {}
+        x_codes = {}
+        x_scales = {}
+        for g in range(PASSES):
+            x_grouped[g] = keep.tile([P, E * C, PACK], BF16, name="x_grouped%d" % g, align_bytes=64)
+            x_codes[g] = keep.tile([P, E * C], U32, name="x_codes%d" % g, align_bytes=64)
+            x_scales[g] = keep.tile([P, E * C], U8, name="x_scales%d" % g, align_bytes=64)
+        w_grouped = {}
         w_codes = {}
         w_scales = {}
-        x_grouped = {}
+        for h in range(PASSES // 2):
+            w_grouped[h] = keep.tile([P, 2, E, N, PACK], BF16, name="w_grouped%d" % h, align_bytes=64)
+            w_codes[h] = keep.tile([P, 2 * E * N], U32, name="w_codes%d" % h, align_bytes=64)
+            w_scales[h] = keep.tile([P, 2 * E * N], U8, name="w_scales%d" % h, align_bytes=64)
+        x_bf = {}
+        biased = {}
+        done = []
+
+        def list_cols(s0, s1):
+            return offsets[:, s0 // 16 : s1 // 16]
+
+        def gather_vector(g, s0, s1):
+            for t in range(PACK):
+                nc.vector.tensor_copy(x_grouped[g][:, s0:s1, t], x_raw[g][:, t, :].indirect(list_cols(s0, s1)))
+
+        def round_whole(g):
+            x_bf[g] = keep.tile([P, PACK, T], BF16, name="x_bf%d" % g)
+            nc.vector.tensor_copy(x_bf[g][:], x_raw[g][:])
+
+        def gather_scalar(g, s0, s1):
+            for t in range(PACK):
+                nc.scalar.activation(x_grouped[g][:, s0:s1, t], x_bf[g][:, t, :].indirect(list_cols(s0, s1)), COPY)
+
+        def quantize(g, s0, s1):
+            nc.vector.quantize_mx(
+                out=x_codes[g][:, s0:s1].bitcast(FP8X4),
+                scales=x_scales[g][:, s0:s1],
+                in_=x_grouped[g][:, s0:s1, :].rearrange("p n t -> p (n t)"),
+            )
 
         def weights_interleave(g):
-            grouped = ring.tile([P, E, N, PACK], BF16, name="w_grouped", align_bytes=64)
-            nc.scalar.copy(out=grouped[:], in_=w_raw[g][:].rearrange("p e j n -> p e n j"))
-            return grouped
+            nc.scalar.copy(out=w_grouped[g // 2][:, g % 2], in_=w_raw[g][:].rearrange("p e j n -> p e n j"))
 
-        def weights_quantize(g, grouped):
-            codes = keep.tile([P, E * N], U32, name="w_codes%d" % g, align_bytes=64)
-            scales = keep.tile([P, E * N], U8, name="w_scales%d" % g, align_bytes=64)
+        def weights_quantize(h):
             nc.vector.quantize_mx(
-                out=codes[:].bitcast(FP8X4),
-                scales=scales[:],
-                in_=grouped[:].rearrange("p e n j -> p (e n j)"),
+                out=w_codes[h][:].bitcast(FP8X4),
+                scales=w_scales[h][:],
+                in_=w_grouped[h][:].rearrange("p g e n j -> p (g e n j)"),
             )
-            w_codes[g] = codes
-            w_scales[g] = scales
 
-        def gather(g, e):
-            picked = ring.tile([P, PACK, C], F32, name="picked")
-            for t in range(PACK):
-                nc.vector.tensor_copy(
-                    picked[:, t, :],
-                    planes[g][t][:].indirect(offsets[:, e * LCOLS : (e + 1) * LCOLS]),
-                )
-            grouped = ring.tile([P, C, PACK], BF16, name="x_grouped", align_bytes=64)
-            nc.scalar.copy(out=grouped[:], in_=picked[:].rearrange("p t n -> p n t"))
-            x_grouped[(g, e)] = grouped
-
-        def multiply(g, e):
-            codes = ring.tile([P, C], U32, name="x_codes", align_bytes=64)
-            scales = ring.tile([P, C], U8, name="x_scales", align_bytes=64)
-            nc.vector.quantize_mx(
-                out=codes[:].bitcast(FP8X4),
-                scales=scales[:],
-                in_=x_grouped[(g, e)][:].rearrange("p n t -> p (n t)"),
-            )
+        def multiply(g, i):
+            s0, s1 = GROUPS[i]
+            e = s0 // C
+            c0 = ((g % 2) * E + e) * N
+            count = len([1 for d in done if d[1] == i])
             nc.tensor.matmul_mx(
-                out=acc[e][:],
-                lhsT=w_codes[g][:, e * N : (e + 1) * N].bitcast(FP8X4),
-                lhsT_scale=w_scales[g][:, e * N : (e + 1) * N],
-                rhs=codes[:].bitcast(FP8X4),
-                rhs_scale=scales[:],
-                start=(g == 0),
-                stop=(g == PASSES - 1),
+                out=acc[i][:],
+                lhsT=w_codes[g // 2][:, c0 : c0 + N].bitcast(FP8X4),
+                lhsT_scale=w_scales[g // 2][:, c0 : c0 + N],
+                rhs=x_codes[g][:, s0:s1].bitcast(FP8X4),
+                rhs_scale=x_scales[g][:, s0:s1],
+                start=(count == 0),
+                stop=(count == PASSES - 1),
             )
+            done.append((g, i))
 
-        biased = {}
+        def add_bias(i):
+            s0, s1 = GROUPS[i]
+            e = s0 // C
+            y = keep.tile([P, s1 - s0], F32, name="y%d" % i)
+            nc.scalar.activation(y[:], acc[i][:], IDENT, bias=b_sb[:, e : e + 1])
+            biased[i] = y
 
-        def add_bias(e):
-            y = keep.tile([P, C], F32, name="y%d" % e)
-            nc.scalar.activation(y[:], acc[e][:], IDENT, bias=b_sb[:, e : e + 1])
-            biased[e] = y
+        def scatter(i):
+            s0, s1 = GROUPS[i]
+            nc.vector.tensor_tensor(result[:].indirect(list_cols(s0, s1)), biased[i][:], gate_sb[:, s0:s1], MULT)
 
-        def scatter(e):
-            nc.vector.tensor_tensor(
-                result[:].indirect(offsets[:, e * LCOLS : (e + 1) * LCOLS]),
-                biased[e][:],
-                gate_sb[:, e * C : (e + 1) * C],
-                MULT,
-            )
-
-        steps = [(0, 0), (0, 1), (1, 0), (1, 1), (2, 0), (3, 0), (2, 1), (3, 1)]
-        before = None
-        for g, e in steps:
-            w_grouped = weights_interleave(g) if e == 0 else None
-            gather(g, e)
-            if w_grouped is not None:
-                weights_quantize(g, w_grouped)
-            if before is not None:
-                multiply(before[0], before[1])
-                if before == (3, 0):
-                    add_bias(0)
-                if before == (2, 1):
-                    scatter(0)
-            before = (g, e)
-        multiply(before[0], before[1])
+        v0, v1, v2 = VECTOR_PASSES
+        f0 = SCALAR_PASSES[0]
+        gather_vector(v0, 0, 256)
+        round_whole(f0)
+        gather_scalar(f0, 0, 256)
+        gather_scalar(f0, 256, 512)
+        gather_vector(v0, 256, 512)
+        weights_interleave(0)
+        weights_interleave(1)
+        gather_vector(v1, 0, 256)
+        quantize(v0, 0, 512)
+        gather_vector(v1, 256, 512)
+        weights_quantize(0)
+        quantize(f0, 0, 512)
+        weights_interleave(2)
+        weights_interleave(3)
+        gather_vector(v2, 0, 256)
+        quantize(v1, 0, 512)
+        weights_quantize(1)
+        for g in (v0, v1, f0):
+            for i in range(3):
+                multiply(g, i)
+        gather_vector(v2, 256, 384)
+        quantize(v2, 0, 256)
+        multiply(v2, 0)
+        add_bias(0)
+        gather_vector(v2, 384, 512)
+        quantize(v2, 256, 384)
+        multiply(v2, 1)
         add_bias(1)
+        scatter(0)
+        quantize(v2, 384, 512)
+        multiply(v2, 2)
+        add_bias(2)
         scatter(1)
+        scatter(2)
+
         nc.sync.dma_start(out, result[:])

@@ -14,15 +14,12 @@ FP8X4 = mybir.dt.float8_e4m3fn_x4
 IDENT = mybir.ActivationFunctionType.Identity
 COPY = mybir.ActivationFunctionType.Copy
 MULT = mybir.AluOpType.mult
+ADD = mybir.AluOpType.add
 
 P = 128
 PACK = 4
 PASSES = K // (P * PACK)
-
-LOADS = [["x",0,4],["x",3,2],["x",1,2],["w",0,1],["w",1,1],["x",2,2],["w",2,1],["w",3,1]]
-SCALAR_PASSES = [3]
-VECTOR_PASSES = [0,1,2]
-GROUPS = [(0, 256), (256, 384), (384, 512)]
+BLOCK = 2048
 
 
 def tile_routed_moe_kernel(tc, xT, w, b, gate, offs, out):
@@ -38,143 +35,146 @@ def tile_routed_moe_kernel(tc, xT, w, b, gate, offs, out):
         warm_in = keep.tile([P, 1], F32, name="warm_in")
         warm_out = keep.tile([P, 1], F32, name="warm_out")
         nc.gpsimd.memset(warm_in[:], 0.0)
-        nc.scalar.activation(warm_out[:], warm_in[:], IDENT)
+        nc.scalar.activation(warm_out[:], warm_in[:], COPY)
 
         x_view = xT.rearrange("(g p t) n -> g p t n", p=P, t=PACK)
         w_view = w.rearrange("e (g p j) n -> g p e j n", p=P, j=PACK)
         x_raw = {}
         w_raw = {}
-        for kind, g, pieces in LOADS:
-            if kind == "x":
-                raw = keep.tile([P, PACK, T], F32, name="x_raw%d" % g)
-                step = PACK // pieces
-                for t0 in range(0, PACK, step):
-                    nc.sync.dma_start(raw[:, t0 : t0 + step, :], x_view[g, :, t0 : t0 + step, :])
-                x_raw[g] = raw
-            else:
-                raw = keep.tile([P, E, PACK, N], F32, name="w_raw%d" % g)
-                nc.sync.dma_start(raw[:], w_view[g])
-                w_raw[g] = raw
-        b_sb = keep.tile([P, E], F32, name="b_sb")
-        nc.sync.dma_start(b_sb[:], b)
-        gate_sb = keep.tile([P, E * C], F32, name="gate_sb")
-        nc.sync.dma_start(gate_sb[:], gate)
-
-        acc = [psum.tile([P, s1 - s0], F32, name="acc%d" % i) for i, (s0, s1) in enumerate(GROUPS)]
-        result = keep.tile([P, T], F32, name="result")
-
-        x_grouped = {}
-        x_codes = {}
-        x_scales = {}
         for g in range(PASSES):
-            x_grouped[g] = keep.tile([P, E * C, PACK], BF16, name="x_grouped%d" % g, align_bytes=64)
-            x_codes[g] = keep.tile([P, E * C], U32, name="x_codes%d" % g, align_bytes=64)
-            x_scales[g] = keep.tile([P, E * C], U8, name="x_scales%d" % g, align_bytes=64)
-        w_grouped = {}
-        w_codes = {}
-        w_scales = {}
-        for h in range(PASSES // 2):
-            w_grouped[h] = keep.tile([P, 2, E, N, PACK], BF16, name="w_grouped%d" % h, align_bytes=64)
-            w_codes[h] = keep.tile([P, 2 * E * N], U32, name="w_codes%d" % h, align_bytes=64)
-            w_scales[h] = keep.tile([P, 2 * E * N], U8, name="w_scales%d" % h, align_bytes=64)
-        x_bf = {}
-        biased = {}
-        done = []
+            x_raw[g] = keep.tile([P, PACK, T], F32, name="x_raw%d" % g)
+            w_raw[g] = keep.tile([P, E, PACK, N], F32, name="w_raw%d" % g)
 
-        def list_cols(s0, s1):
-            return offsets[:, s0 // 16 : s1 // 16]
+        def load_x(g, t0, t1):
+            nc.sync.dma_start(x_raw[g][:, t0:t1, :], x_view[g, :, t0:t1, :])
 
-        def gather_vector(g, s0, s1):
-            for t in range(PACK):
-                nc.vector.tensor_copy(x_grouped[g][:, s0:s1, t], x_raw[g][:, t, :].indirect(list_cols(s0, s1)))
+        def load_w(g):
+            nc.sync.dma_start(w_raw[g][:], w_view[g])
 
-        def round_whole(g):
-            x_bf[g] = keep.tile([P, PACK, T], BF16, name="x_bf%d" % g)
-            nc.vector.tensor_copy(x_bf[g][:], x_raw[g][:])
+        acc = [psum.tile([P, C], F32, name="acc%d" % e) for e in range(E)]
+        result = keep.tile([P, T], F32, name="result")
+        b_sb = keep.tile([P, E], F32, name="b_sb")
+        gate_sb = keep.tile([P, E * C], F32, name="gate_sb")
+        x_bf = keep.tile([P, PACK, T], BF16, name="x_bf")
 
-        def gather_scalar(g, s0, s1):
-            for t in range(PACK):
-                nc.scalar.activation(x_grouped[g][:, s0:s1, t], x_bf[g][:, t, :].indirect(list_cols(s0, s1)), COPY)
+        early = keep.tile([P, 2 * BLOCK], BF16, name="early", align_bytes=64)
+        early_codes = keep.tile([P, 2 * BLOCK // PACK], U32, name="early_codes", align_bytes=64)
+        early_scales = keep.tile([P, 2 * BLOCK // PACK], U8, name="early_scales", align_bytes=64)
+        late = keep.tile([P, 4 * BLOCK], BF16, name="late", align_bytes=64)
+        late_codes = keep.tile([P, 4 * BLOCK // PACK], U32, name="late_codes", align_bytes=64)
+        late_scales = keep.tile([P, 4 * BLOCK // PACK], U8, name="late_scales", align_bytes=64)
 
-        def quantize(g, s0, s1):
-            nc.vector.quantize_mx(
-                out=x_codes[g][:, s0:s1].bitcast(FP8X4),
-                scales=x_scales[g][:, s0:s1],
-                in_=x_grouped[g][:, s0:s1, :].rearrange("p n t -> p (n t)"),
-            )
+        def token_base(g, e):
+            if g < 2:
+                return early, early_codes, early_scales, g * T + e * C
+            return late, late_codes, late_scales, {(3, 0): 2, (2, 0): 3, (2, 1): 4, (3, 1): 5}[(g, e)] * C
+
+        def weight_base(g, e):
+            return 3 * e * T + g * N
+
+        def grouped(g, e0, e1, t):
+            tile, codes, scales, c0 = token_base(g, e0)
+            return tile[:, c0 * PACK : (c0 + (e1 - e0) * C) * PACK].rearrange("p (n t) -> p n t", t=PACK)[:, :, t]
+
+        def list_cols(e0, e1):
+            return offsets[:, e0 * C // 16 : e1 * C // 16]
+
+        def gather_vector(g, t, e0, e1):
+            if e1 - e0 == E:
+                window = x_raw[g][:, t : t + 2, :].rearrange("p t n -> p (t n)")
+            else:
+                window = x_raw[g][:, t, :]
+            nc.vector.tensor_copy(grouped(g, e0, e1, t), window.indirect(list_cols(e0, e1)))
+
+        def round_scalar(g, t0, t1):
+            nc.scalar.copy(out=x_bf[:, t0:t1, :], in_=x_raw[g][:, t0:t1, :])
+
+        def gather_scalar(g, t, e):
+            nc.scalar.activation(grouped(g, e, e + 1, t), x_bf[:, t, :].indirect(list_cols(e, e + 1)), COPY)
 
         def weights_interleave(g):
-            nc.scalar.copy(out=w_grouped[g // 2][:, g % 2], in_=w_raw[g][:].rearrange("p e j n -> p e n j"))
+            nc.scalar.copy(
+                out=late[:]
+                .rearrange("p (a c) -> p a c", c=BLOCK)[:, 0:4:3, g * N * PACK : (g + 1) * N * PACK]
+                .rearrange("p e (n j) -> p e n j", j=PACK),
+                in_=w_raw[g][:].rearrange("p e j n -> p e n j"),
+            )
 
-        def weights_quantize(h):
+        def quantize(tile, codes, scales, c0, c1):
             nc.vector.quantize_mx(
-                out=w_codes[h][:].bitcast(FP8X4),
-                scales=w_scales[h][:],
-                in_=w_grouped[h][:].rearrange("p g e n j -> p (g e n j)"),
+                out=codes[:, c0 // PACK : c1 // PACK].bitcast(FP8X4),
+                scales=scales[:, c0 // PACK : c1 // PACK],
+                in_=tile[:, c0:c1],
             )
 
-        def multiply(g, i):
-            s0, s1 = GROUPS[i]
-            e = s0 // C
-            c0 = ((g % 2) * E + e) * N
-            count = len([1 for d in done if d[1] == i])
-            nc.tensor.matmul_mx(
-                out=acc[i][:],
-                lhsT=w_codes[g // 2][:, c0 : c0 + N].bitcast(FP8X4),
-                lhsT_scale=w_scales[g // 2][:, c0 : c0 + N],
-                rhs=x_codes[g][:, s0:s1].bitcast(FP8X4),
-                rhs_scale=x_scales[g][:, s0:s1],
-                start=(count == 0),
-                stop=(count == PASSES - 1),
+        def multiply(e):
+            for g in range(PASSES):
+                tile, codes, scales, c0 = token_base(g, e)
+                w0 = weight_base(g, e)
+                nc.tensor.matmul_mx(
+                    out=acc[e][:],
+                    lhsT=late_codes[:, w0 : w0 + N].bitcast(FP8X4),
+                    lhsT_scale=late_scales[:, w0 : w0 + N],
+                    rhs=codes[:, c0 : c0 + C].bitcast(FP8X4),
+                    rhs_scale=scales[:, c0 : c0 + C],
+                    start=(g == 0),
+                    stop=(g == PASSES - 1),
+                )
+
+        def finish(e):
+            y = keep.tile([P, C], F32, name="y%d" % e)
+            nc.vector.scalar_tensor_tensor(
+                out=y[:], in0=acc[e][:], scalar=b_sb[:, e : e + 1], in1=gate_sb[:, e * C : (e + 1) * C], op0=ADD, op1=MULT
             )
-            done.append((g, i))
+            nc.vector.tensor_copy(result[:].indirect(list_cols(e, e + 1)), y[:])
 
-        def add_bias(i):
-            s0, s1 = GROUPS[i]
-            e = s0 // C
-            y = keep.tile([P, s1 - s0], F32, name="y%d" % i)
-            nc.scalar.activation(y[:], acc[i][:], IDENT, bias=b_sb[:, e : e + 1])
-            biased[i] = y
+        load_x(0, 0, 1)
+        load_x(0, 1, 2)
+        load_x(3, 0, 2)
+        load_x(0, 2, 3)
+        load_x(0, 3, 4)
+        load_x(3, 2, 4)
+        load_x(1, 0, 2)
+        load_x(1, 2, 4)
+        load_w(0)
+        load_w(1)
+        load_x(2, 0, 2)
+        load_w(2)
+        load_x(2, 2, 4)
+        load_w(3)
+        nc.sync.dma_start(b_sb[:], b)
+        nc.sync.dma_start(gate_sb[:], gate)
 
-        def scatter(i):
-            s0, s1 = GROUPS[i]
-            nc.vector.tensor_tensor(result[:].indirect(list_cols(s0, s1)), biased[i][:], gate_sb[:, s0:s1], MULT)
+        for t0 in (0, 2):
+            round_scalar(3, t0, t0 + 2)
+            for t in (t0, t0 + 1):
+                gather_scalar(3, t, 0)
+        for g in range(PASSES):
+            weights_interleave(g)
+        for t in range(PACK):
+            gather_scalar(3, t, 1)
 
-        v0, v1, v2 = VECTOR_PASSES
-        f0 = SCALAR_PASSES[0]
-        gather_vector(v0, 0, 256)
-        round_whole(f0)
-        gather_scalar(f0, 0, 256)
-        gather_scalar(f0, 256, 512)
-        gather_vector(v0, 256, 512)
-        weights_interleave(0)
-        weights_interleave(1)
-        gather_vector(v1, 0, 256)
-        quantize(v0, 0, 512)
-        gather_vector(v1, 256, 512)
-        weights_quantize(0)
-        quantize(f0, 0, 512)
-        weights_interleave(2)
-        weights_interleave(3)
-        gather_vector(v2, 0, 256)
-        quantize(v1, 0, 512)
-        weights_quantize(1)
-        for g in (v0, v1, f0):
-            for i in range(3):
-                multiply(g, i)
-        gather_vector(v2, 256, 384)
-        quantize(v2, 0, 256)
-        multiply(v2, 0)
-        add_bias(0)
-        gather_vector(v2, 384, 512)
-        quantize(v2, 256, 384)
-        multiply(v2, 1)
-        add_bias(1)
-        scatter(0)
-        quantize(v2, 384, 512)
-        multiply(v2, 2)
-        add_bias(2)
-        scatter(1)
-        scatter(2)
+        for t in (0, 1):
+            for e in range(E):
+                gather_vector(0, t, e, e + 1)
+        gather_vector(0, 2, 0, E)
+        for e in range(E):
+            gather_vector(0, 3, e, e + 1)
+        for t in range(3):
+            gather_vector(1, t, 0, E)
+        for e in range(E):
+            gather_vector(1, 3, e, e + 1)
+        gather_vector(2, 0, 0, E)
+        quantize(early, early_codes, early_scales, 0, 2 * BLOCK)
+        gather_vector(2, 1, 0, E)
+        gather_vector(2, 2, 0, E)
+        gather_vector(2, 3, 0, 1)
+        quantize(late, late_codes, late_scales, 0, 2 * BLOCK)
+        multiply(0)
+        gather_vector(2, 3, 1, 2)
+        quantize(late, late_codes, late_scales, 2 * BLOCK, 4 * BLOCK)
+        multiply(1)
+        finish(0)
+        finish(1)
 
         nc.sync.dma_start(out, result[:])

@@ -92,8 +92,8 @@ def tile_routed_moe_kernel(tc, xT, w, b, gate, offs, out):
         def gather_scalar(g, t, e):
             nc.scalar.activation(grouped(g, e, e + 1, t), x_bf[:, t, :].indirect(list_cols(e, e + 1)), COPY)
 
-        def weights_interleave(g):
-            nc.scalar.copy(
+        def weights_interleave(copy, g):
+            copy(
                 out=late[:]
                 .rearrange("p (a c) -> p a c", c=BLOCK)[:, 0:4:3, g * N * PACK : (g + 1) * N * PACK]
                 .rearrange("p e (n j) -> p e n j", j=PACK),
@@ -136,12 +136,10 @@ def tile_routed_moe_kernel(tc, xT, w, b, gate, offs, out):
         load_x(3, 2, 4)
         load_x(1, 0, 2)
         load_x(1, 2, 4)
-        load_w(0)
-        load_w(1)
         load_x(2, 0, 2)
-        load_w(2)
         load_x(2, 2, 4)
-        load_w(3)
+        for g in range(PASSES):
+            load_w(g)
         nc.sync.dma_start(b_sb[:], b)
         nc.sync.dma_start(gate_sb[:], gate)
 
@@ -149,8 +147,8 @@ def tile_routed_moe_kernel(tc, xT, w, b, gate, offs, out):
             round_scalar(3, t0, t0 + 2)
             for t in (t0, t0 + 1):
                 gather_scalar(3, t, 0)
-        for g in range(PASSES):
-            weights_interleave(g)
+        for g in (0, 1):
+            weights_interleave(nc.scalar.copy, g)
         for t in range(PACK):
             gather_scalar(3, t, 1)
 
@@ -169,6 +167,8 @@ def tile_routed_moe_kernel(tc, xT, w, b, gate, offs, out):
         gather_vector(2, 1, 0, E)
         gather_vector(2, 2, 0, E)
         gather_vector(2, 3, 0, 1)
+        for g in (2, 3):
+            weights_interleave(nc.vector.tensor_copy, g)
         quantize(late, late_codes, late_scales, 0, 2 * BLOCK)
         multiply(0)
         gather_vector(2, 3, 1, 2)

@@ -11,7 +11,6 @@ U32 = mybir.dt.uint32
 U16 = mybir.dt.uint16
 U8 = mybir.dt.uint8
 FP8X4 = mybir.dt.float8_e4m3fn_x4
-IDENT = mybir.ActivationFunctionType.Identity
 COPY = mybir.ActivationFunctionType.Copy
 MULT = mybir.AluOpType.mult
 ADD = mybir.AluOpType.add
@@ -20,6 +19,7 @@ P = 128
 PACK = 4
 PASSES = K // (P * PACK)
 BLOCK = 2048
+SPLIT = 384
 
 
 def tile_routed_moe_kernel(tc, xT, w, b, gate, offs, out):
@@ -41,9 +41,14 @@ def tile_routed_moe_kernel(tc, xT, w, b, gate, offs, out):
         w_view = w.rearrange("e (g p j) n -> g p e j n", p=P, j=PACK)
         x_raw = {}
         w_raw = {}
+        x_bf = {}
         for g in range(PASSES):
-            x_raw[g] = keep.tile([P, PACK, T], F32, name="x_raw%d" % g)
+            x_raw[g] = keep.tile([P, PACK + 1, T], F32, name="x_raw%d" % g)
             w_raw[g] = keep.tile([P, E, PACK, N], F32, name="w_raw%d" % g)
+        for g in (0, 1):
+            nc.gpsimd.memset(x_raw[g][:, PACK, :], 0.0)
+        for g in (2, 3):
+            x_bf[g] = keep.tile([P, PACK, T], BF16, name="x_bf%d" % g)
 
         def load_x(g, t0, t1):
             nc.sync.dma_start(x_raw[g][:, t0:t1, :], x_view[g, :, t0:t1, :])
@@ -55,7 +60,6 @@ def tile_routed_moe_kernel(tc, xT, w, b, gate, offs, out):
         result = keep.tile([P, T], F32, name="result")
         b_sb = keep.tile([P, E], F32, name="b_sb")
         gate_sb = keep.tile([P, E * C], F32, name="gate_sb")
-        x_bf = keep.tile([P, PACK, T], BF16, name="x_bf")
 
         early = keep.tile([P, 2 * BLOCK], BF16, name="early", align_bytes=64)
         early_codes = keep.tile([P, 2 * BLOCK // PACK], U32, name="early_codes", align_bytes=64)
@@ -64,40 +68,46 @@ def tile_routed_moe_kernel(tc, xT, w, b, gate, offs, out):
         late_codes = keep.tile([P, 4 * BLOCK // PACK], U32, name="late_codes", align_bytes=64)
         late_scales = keep.tile([P, 4 * BLOCK // PACK], U8, name="late_scales", align_bytes=64)
 
-        def token_base(g, e):
+        def token_base(g, s):
             if g < 2:
-                return early, early_codes, early_scales, g * T + e * C
-            return late, late_codes, late_scales, {(3, 0): 2, (2, 0): 3, (2, 1): 4, (3, 1): 5}[(g, e)] * C
+                return early, early_codes, early_scales, g * T + s
+            if g == 2:
+                return late, late_codes, late_scales, 3 * C + s
+            return late, late_codes, late_scales, (2 * C + s) if s < C else (4 * C + s)
 
         def weight_base(g, e):
             return 3 * e * T + g * N
 
-        def grouped(g, e0, e1, t):
-            tile, codes, scales, c0 = token_base(g, e0)
-            return tile[:, c0 * PACK : (c0 + (e1 - e0) * C) * PACK].rearrange("p (n t) -> p n t", t=PACK)[:, :, t]
+        def grouped(g, s0, s1, t):
+            tile, codes, scales, c0 = token_base(g, s0)
+            return tile[:, c0 * PACK : (c0 + s1 - s0) * PACK].rearrange("p (n t) -> p n t", t=PACK)[:, :, t]
 
-        def list_cols(e0, e1):
-            return offsets[:, e0 * C // 16 : e1 * C // 16]
+        def list_cols(s0, s1):
+            return offsets[:, s0 // 16 : s1 // 16]
 
-        def gather_vector(g, t, e0, e1):
-            if e1 - e0 == E:
+        def gather_vector(g, t, s0, s1):
+            if s1 - s0 == T:
                 window = x_raw[g][:, t : t + 2, :].rearrange("p t n -> p (t n)")
             else:
                 window = x_raw[g][:, t, :]
-            nc.vector.tensor_copy(grouped(g, e0, e1, t), window.indirect(list_cols(e0, e1)))
+            nc.vector.tensor_copy(grouped(g, s0, s1, t), window.indirect(list_cols(s0, s1)))
 
         def round_scalar(g, t0, t1):
-            nc.scalar.copy(out=x_bf[:, t0:t1, :], in_=x_raw[g][:, t0:t1, :])
+            nc.scalar.copy(out=x_bf[g][:, t0:t1, :], in_=x_raw[g][:, t0:t1, :])
 
-        def gather_scalar(g, t, e):
-            nc.scalar.activation(grouped(g, e, e + 1, t), x_bf[:, t, :].indirect(list_cols(e, e + 1)), COPY)
+        def gather_scalar(g, t, s0, s1):
+            nc.scalar.activation(grouped(g, s0, s1, t), x_bf[g][:, t, :].indirect(list_cols(s0, s1)), COPY)
 
-        def weights_interleave(copy, g):
-            copy(
+        def weights_interleave(g):
+            nc.gpsimd.tensor_scalar(
                 out=late[:]
                 .rearrange("p (a c) -> p a c", c=BLOCK)[:, 0:4:3, g * N * PACK : (g + 1) * N * PACK]
                 .rearrange("p e (n j) -> p e n j", j=PACK),
-                in_=w_raw[g][:].rearrange("p e j n -> p e n j"),
+                in0=w_raw[g][:].rearrange("p e j n -> p e n j"),
+                scalar1=1.0,
+                scalar2=0.0,
+                op0=MULT,
+                op1=ADD,
             )
 
         def quantize(tile, codes, scales, c0, c1):
@@ -109,7 +119,7 @@ def tile_routed_moe_kernel(tc, xT, w, b, gate, offs, out):
 
         def multiply(e):
             for g in range(PASSES):
-                tile, codes, scales, c0 = token_base(g, e)
+                tile, codes, scales, c0 = token_base(g, e * C)
                 w0 = weight_base(g, e)
                 nc.tensor.matmul_mx(
                     out=acc[e][:],
@@ -126,7 +136,7 @@ def tile_routed_moe_kernel(tc, xT, w, b, gate, offs, out):
             nc.vector.scalar_tensor_tensor(
                 out=y[:], in0=acc[e][:], scalar=b_sb[:, e : e + 1], in1=gate_sb[:, e * C : (e + 1) * C], op0=ADD, op1=MULT
             )
-            nc.vector.tensor_copy(result[:].indirect(list_cols(e, e + 1)), y[:])
+            nc.vector.tensor_copy(result[:].indirect(list_cols(e * C, (e + 1) * C)), y[:])
 
         load_x(0, 0, 1)
         load_x(0, 1, 2)
@@ -136,42 +146,44 @@ def tile_routed_moe_kernel(tc, xT, w, b, gate, offs, out):
         load_x(3, 2, 4)
         load_x(1, 0, 2)
         load_x(1, 2, 4)
+        load_w(0)
+        load_w(1)
         load_x(2, 0, 2)
         load_x(2, 2, 4)
-        for g in range(PASSES):
-            load_w(g)
+        load_w(2)
+        load_w(3)
         nc.sync.dma_start(b_sb[:], b)
         nc.sync.dma_start(gate_sb[:], gate)
+
+        for g in range(PASSES):
+            weights_interleave(g)
 
         for t0 in (0, 2):
             round_scalar(3, t0, t0 + 2)
             for t in (t0, t0 + 1):
-                gather_scalar(3, t, 0)
-        for g in (0, 1):
-            weights_interleave(nc.scalar.copy, g)
+                gather_scalar(3, t, 0, C)
         for t in range(PACK):
-            gather_scalar(3, t, 1)
+            gather_scalar(3, t, C, T)
+        for t0 in (0, 2):
+            round_scalar(2, t0, t0 + 2)
+            for t in (t0, t0 + 1):
+                gather_scalar(2, t, SPLIT, T)
 
         for t in (0, 1):
             for e in range(E):
-                gather_vector(0, t, e, e + 1)
-        gather_vector(0, 2, 0, E)
-        for e in range(E):
-            gather_vector(0, 3, e, e + 1)
-        for t in range(3):
-            gather_vector(1, t, 0, E)
-        for e in range(E):
-            gather_vector(1, 3, e, e + 1)
-        gather_vector(2, 0, 0, E)
+                gather_vector(0, t, e * C, (e + 1) * C)
+        for t in (2, 3):
+            gather_vector(0, t, 0, T)
+        for t in range(PACK):
+            gather_vector(1, t, 0, T)
+        gather_vector(2, 0, 0, SPLIT)
         quantize(early, early_codes, early_scales, 0, 2 * BLOCK)
-        gather_vector(2, 1, 0, E)
-        gather_vector(2, 2, 0, E)
-        gather_vector(2, 3, 0, 1)
-        for g in (2, 3):
-            weights_interleave(nc.vector.tensor_copy, g)
+        gather_vector(2, 1, 0, SPLIT)
+        gather_vector(2, 2, 0, SPLIT)
+        gather_vector(2, 3, 0, C)
         quantize(late, late_codes, late_scales, 0, 2 * BLOCK)
         multiply(0)
-        gather_vector(2, 3, 1, 2)
+        gather_vector(2, 3, C, SPLIT)
         quantize(late, late_codes, late_scales, 2 * BLOCK, 4 * BLOCK)
         multiply(1)
         finish(0)

@@ -18,8 +18,8 @@ ADD = mybir.AluOpType.add
 P = 128
 PACK = 4
 PASSES = K // (P * PACK)
-BLOCK = 2048
-SPLIT = 384
+UNIT = C * PACK
+WUNIT = N * PACK
 
 
 def tile_routed_moe_kernel(tc, xT, w, b, gate, offs, out):
@@ -38,155 +38,153 @@ def tile_routed_moe_kernel(tc, xT, w, b, gate, offs, out):
         nc.scalar.activation(warm_out[:], warm_in[:], COPY)
 
         x_view = xT.rearrange("(g p t) n -> g p t n", p=P, t=PACK)
-        w_view = w.rearrange("e (g p j) n -> g p e j n", p=P, j=PACK)
-        x_raw = {}
-        w_raw = {}
-        x_bf = {}
-        for g in range(PASSES):
-            x_raw[g] = keep.tile([P, PACK + 1, T], F32, name="x_raw%d" % g)
-            w_raw[g] = keep.tile([P, E, PACK, N], F32, name="w_raw%d" % g)
-        for g in (0, 1):
-            nc.gpsimd.memset(x_raw[g][:, PACK, :], 0.0)
+        w_view = w.rearrange("e (g p j) n -> e p g j n", p=P, j=PACK)
+
+        xv = keep.tile([P, 2 * PACK + 1, T], F32, name="xv")
+        nc.gpsimd.memset(xv[:, 2 * PACK, :], 0.0)
+        place = {(0, 0): 7, (0, 1): 6, (0, 2): 4, (0, 3): 5, (1, 0): 2, (1, 1): 3, (1, 2): 0, (1, 3): 1}
+        xs = {}
+        xb = {}
         for g in (2, 3):
-            x_bf[g] = keep.tile([P, PACK, T], BF16, name="x_bf%d" % g)
+            xs[g] = keep.tile([P, PACK, T], F32, name="xs%d" % g)
+            xb[g] = keep.tile([P, PACK, T], BF16, name="xb%d" % g)
+        w_raw = keep.tile([P, E, PASSES, PACK, N], F32, name="w_raw")
 
-        def load_x(g, t0, t1):
-            nc.sync.dma_start(x_raw[g][:, t0:t1, :], x_view[g, :, t0:t1, :])
-
-        def load_w(g):
-            nc.sync.dma_start(w_raw[g][:], w_view[g])
-
-        acc = [psum.tile([P, C], F32, name="acc%d" % e) for e in range(E)]
+        acc = [psum.tile([P, 2 * C], F32, name="acc%d" % e) for e in range(E)]
         result = keep.tile([P, T], F32, name="result")
         b_sb = keep.tile([P, E], F32, name="b_sb")
         gate_sb = keep.tile([P, E * C], F32, name="gate_sb")
 
-        early = keep.tile([P, 2 * BLOCK], BF16, name="early", align_bytes=64)
-        early_codes = keep.tile([P, 2 * BLOCK // PACK], U32, name="early_codes", align_bytes=64)
-        early_scales = keep.tile([P, 2 * BLOCK // PACK], U8, name="early_scales", align_bytes=64)
-        late = keep.tile([P, 4 * BLOCK], BF16, name="late", align_bytes=64)
-        late_codes = keep.tile([P, 4 * BLOCK // PACK], U32, name="late_codes", align_bytes=64)
-        late_scales = keep.tile([P, 4 * BLOCK // PACK], U8, name="late_scales", align_bytes=64)
+        token_piece = {(0, 0): 0, (0, 1): 1, (2, 0): 2, (2, 1): 3, (1, 0): 4, (1, 1): 5, (3, 0): 9, (3, 1): 11}
+        weight_piece = {(0, 0): 6, (1, 0): 7, (0, 1): 8, (1, 1): 10}
+        PIECES = 12
+        row = keep.tile([P, PIECES * UNIT], BF16, name="row", align_bytes=64)
+        codes = keep.tile([P, PIECES * C], U32, name="codes", align_bytes=64)
+        scales = keep.tile([P, PIECES * C], U8, name="scales", align_bytes=64)
 
-        def token_base(g, s):
+        def load_x(g, t0, t1):
             if g < 2:
-                return early, early_codes, early_scales, g * T + s
-            if g == 2:
-                return late, late_codes, late_scales, 3 * C + s
-            return late, late_codes, late_scales, (2 * C + s) if s < C else (4 * C + s)
-
-        def weight_base(g, e):
-            return 3 * e * T + g * N
-
-        def grouped(g, s0, s1, t):
-            tile, codes, scales, c0 = token_base(g, s0)
-            return tile[:, c0 * PACK : (c0 + s1 - s0) * PACK].rearrange("p (n t) -> p n t", t=PACK)[:, :, t]
-
-        def list_cols(s0, s1):
-            return offsets[:, s0 // 16 : s1 // 16]
-
-        def gather_vector(g, t, s0, s1):
-            if s1 - s0 == T:
-                window = x_raw[g][:, t : t + 2, :].rearrange("p t n -> p (t n)")
+                q = place[(g, t0)]
+                nc.sync.dma_start(xv[:, q : q + t1 - t0, :], x_view[g, :, t0:t1, :])
             else:
-                window = x_raw[g][:, t, :]
-            nc.vector.tensor_copy(grouped(g, s0, s1, t), window.indirect(list_cols(s0, s1)))
+                nc.sync.dma_start(xs[g][:, t0:t1, :], x_view[g, :, t0:t1, :])
 
-        def round_scalar(g, t0, t1):
-            nc.scalar.copy(out=x_bf[g][:, t0:t1, :], in_=x_raw[g][:, t0:t1, :])
+        def load_w(e, h):
+            nc.sync.dma_start(w_raw[:, e, 2 * h : 2 * h + 2], w_view[e, :, 2 * h : 2 * h + 2])
 
-        def gather_scalar(g, t, s0, s1):
-            nc.scalar.activation(grouped(g, s0, s1, t), x_bf[g][:, t, :].indirect(list_cols(s0, s1)), COPY)
-
-        def weights_interleave(g):
+        def cast(g, t0, t1):
             nc.gpsimd.tensor_scalar(
-                out=late[:]
-                .rearrange("p (a c) -> p a c", c=BLOCK)[:, 0:4:3, g * N * PACK : (g + 1) * N * PACK]
-                .rearrange("p e (n j) -> p e n j", j=PACK),
-                in0=w_raw[g][:].rearrange("p e j n -> p e n j"),
+                out=xb[g][:, t0:t1, :], in0=xs[g][:, t0:t1, :], scalar1=1.0, scalar2=0.0, op0=MULT, op1=ADD
+            )
+
+        def weights_interleave(e, h):
+            c0 = weight_piece[(e, h)] * UNIT
+            nc.gpsimd.tensor_scalar(
+                out=row[:, c0 : c0 + UNIT].rearrange("p (g n j) -> p g n j", g=2, j=PACK),
+                in0=w_raw[:, e, 2 * h : 2 * h + 2].rearrange("p g j n -> p g n j"),
                 scalar1=1.0,
                 scalar2=0.0,
                 op0=MULT,
                 op1=ADD,
             )
 
-        def quantize(tile, codes, scales, c0, c1):
+        def grouped(g, e0, e1, t):
+            c0 = token_piece[(g, e0)] * UNIT
+            c1 = c0 + (e1 - e0) * UNIT
+            return row[:, c0:c1].rearrange("p (n t) -> p n t", t=PACK)[:, :, t]
+
+        def list_cols(e0, e1):
+            return offsets[:, e0 * C // 16 : e1 * C // 16]
+
+        def gather_vector(g, t):
+            q = place[(g, t)]
+            window = xv[:, q : q + 2, :].rearrange("p t n -> p (t n)")
+            nc.vector.tensor_copy(grouped(g, 0, E, t), window.indirect(list_cols(0, E)))
+
+        def gather_scalar(g, t, e):
+            nc.scalar.activation(grouped(g, e, e + 1, t), xb[g][:, t, :].indirect(list_cols(e, e + 1)), COPY)
+
+        def quantize(u0, u1):
             nc.vector.quantize_mx(
-                out=codes[:, c0 // PACK : c1 // PACK].bitcast(FP8X4),
-                scales=scales[:, c0 // PACK : c1 // PACK],
-                in_=tile[:, c0:c1],
+                out=codes[:, u0 * C : u1 * C].bitcast(FP8X4),
+                scales=scales[:, u0 * C : u1 * C],
+                in_=row[:, u0 * UNIT : u1 * UNIT],
             )
 
-        def multiply(e):
-            for g in range(PASSES):
-                tile, codes, scales, c0 = token_base(g, e * C)
-                w0 = weight_base(g, e)
-                nc.tensor.matmul_mx(
-                    out=acc[e][:],
-                    lhsT=late_codes[:, w0 : w0 + N].bitcast(FP8X4),
-                    lhsT_scale=late_scales[:, w0 : w0 + N],
-                    rhs=codes[:, c0 : c0 + C].bitcast(FP8X4),
-                    rhs_scale=scales[:, c0 : c0 + C],
-                    start=(g == 0),
-                    stop=(g == PASSES - 1),
-                )
+        def multiply(e, g):
+            c0 = token_piece[(g, e)] * C
+            w0 = weight_piece[(e, g // 2)] * C + (g % 2) * N
+            nc.tensor.matmul_mx(
+                out=acc[e][:, 0:C],
+                lhsT=codes[:, w0 : w0 + N].bitcast(FP8X4),
+                lhsT_scale=scales[:, w0 : w0 + N],
+                rhs=codes[:, c0 : c0 + C].bitcast(FP8X4),
+                rhs_scale=scales[:, c0 : c0 + C],
+                start=(g == 0),
+                stop=(g == PASSES - 1),
+            )
 
         def finish(e):
             y = keep.tile([P, C], F32, name="y%d" % e)
             nc.vector.scalar_tensor_tensor(
-                out=y[:], in0=acc[e][:], scalar=b_sb[:, e : e + 1], in1=gate_sb[:, e * C : (e + 1) * C], op0=ADD, op1=MULT
+                out=y[:], in0=acc[e][:, 0:C], scalar=b_sb[:, e : e + 1], in1=gate_sb[:, e * C : (e + 1) * C], op0=ADD, op1=MULT
             )
-            nc.vector.tensor_copy(result[:].indirect(list_cols(e * C, (e + 1) * C)), y[:])
+            nc.vector.tensor_copy(result[:].indirect(list_cols(e, e + 1)), y[:])
 
         load_x(0, 0, 1)
+        load_x(2, 0, 1)
         load_x(0, 1, 2)
-        load_x(3, 0, 2)
-        load_x(0, 2, 3)
-        load_x(0, 3, 4)
-        load_x(3, 2, 4)
-        load_x(1, 0, 2)
-        load_x(1, 2, 4)
-        load_w(0)
-        load_w(1)
-        load_x(2, 0, 2)
+        load_x(2, 1, 2)
+        load_x(0, 2, 4)
         load_x(2, 2, 4)
-        load_w(2)
-        load_w(3)
-        nc.sync.dma_start(b_sb[:], b)
+        load_x(1, 0, 2)
+        load_x(3, 0, 2)
+        load_x(1, 2, 4)
+        load_x(3, 2, 4)
+        load_w(0, 0)
+        load_w(1, 0)
+        load_w(0, 1)
+        load_w(1, 1)
         nc.sync.dma_start(gate_sb[:], gate)
+        nc.sync.dma_start(b_sb[:], b)
 
-        for g in range(PASSES):
-            weights_interleave(g)
+        cast(2, 0, 1)
+        cast(2, 1, 2)
+        cast(2, 2, 4)
+        cast(3, 0, 2)
+        cast(3, 2, 3)
+        cast(3, 3, 4)
+        weights_interleave(0, 0)
+        weights_interleave(1, 0)
+        weights_interleave(0, 1)
+        weights_interleave(1, 1)
 
-        for t0 in (0, 2):
-            round_scalar(3, t0, t0 + 2)
-            for t in (t0, t0 + 1):
-                gather_scalar(3, t, 0, C)
         for t in range(PACK):
-            gather_scalar(3, t, C, T)
-        for t0 in (0, 2):
-            round_scalar(2, t0, t0 + 2)
-            for t in (t0, t0 + 1):
-                gather_scalar(2, t, SPLIT, T)
-
-        for t in (0, 1):
             for e in range(E):
-                gather_vector(0, t, e * C, (e + 1) * C)
-        for t in (2, 3):
-            gather_vector(0, t, 0, T)
+                gather_scalar(2, t, e)
+        for e in range(E):
+            for t in range(PACK):
+                gather_scalar(3, t, e)
+
         for t in range(PACK):
-            gather_vector(1, t, 0, T)
-        gather_vector(2, 0, 0, SPLIT)
-        quantize(early, early_codes, early_scales, 0, 2 * BLOCK)
-        gather_vector(2, 1, 0, SPLIT)
-        gather_vector(2, 2, 0, SPLIT)
-        gather_vector(2, 3, 0, C)
-        quantize(late, late_codes, late_scales, 0, 2 * BLOCK)
-        multiply(0)
-        gather_vector(2, 3, C, SPLIT)
-        quantize(late, late_codes, late_scales, 2 * BLOCK, 4 * BLOCK)
-        multiply(1)
+            gather_vector(0, t)
+        for t in (0, 1):
+            gather_vector(1, t)
+        quantize(0, 2)
+        for t in (2, 3):
+            gather_vector(1, t)
+        quantize(2, 6)
+        quantize(6, 8)
+        for e in range(E):
+            for g in (0, 1):
+                multiply(e, g)
+        quantize(8, 10)
+        for g in (2, 3):
+            multiply(0, g)
         finish(0)
+        quantize(10, 12)
+        for g in (2, 3):
+            multiply(1, g)
         finish(1)
 
         nc.sync.dma_start(out, result[:])

@@ -42,7 +42,7 @@ def tile_routed_moe_kernel(tc, xT, w, b, gate, offs, out):
 
         xv = keep.tile([P, 2 * PACK + 1, T], F32, name="xv")
         nc.gpsimd.memset(xv[:, 2 * PACK, :], 0.0)
-        place = {(0, 0): 7, (0, 1): 6, (0, 2): 4, (0, 3): 5, (1, 0): 2, (1, 1): 3, (1, 2): 0, (1, 3): 1}
+        place = {(0, 0): 7, (0, 1): 6, (0, 2): 5, (0, 3): 4, (1, 0): 2, (1, 1): 3, (1, 2): 0, (1, 3): 1}
         xs = {}
         xb = {}
         for g in (2, 3):
@@ -55,8 +55,8 @@ def tile_routed_moe_kernel(tc, xT, w, b, gate, offs, out):
         b_sb = keep.tile([P, E], F32, name="b_sb")
         gate_sb = keep.tile([P, E * C], F32, name="gate_sb")
 
-        token_piece = {(0, 0): 0, (0, 1): 1, (2, 0): 2, (2, 1): 3, (1, 0): 4, (1, 1): 5, (3, 0): 9, (3, 1): 11}
-        weight_piece = {(0, 0): 6, (1, 0): 7, (0, 1): 8, (1, 1): 10}
+        token_piece = {(0, 0): 0, (0, 1): 1, (2, 0): 2, (2, 1): 3, (1, 0): 4, (1, 1): 5, (3, 0): 8, (3, 1): 11}
+        weight_piece = {(0, 0): 6, (0, 1): 7, (1, 0): 9, (1, 1): 10}
         PIECES = 12
         row = keep.tile([P, PIECES * UNIT], BF16, name="row", align_bytes=64)
         codes = keep.tile([P, PIECES * C], U32, name="codes", align_bytes=64)
@@ -101,8 +101,9 @@ def tile_routed_moe_kernel(tc, xT, w, b, gate, offs, out):
             window = xv[:, q : q + 2, :].rearrange("p t n -> p (t n)")
             nc.vector.tensor_copy(grouped(g, 0, E, t), window.indirect(list_cols(0, E)))
 
-        def gather_scalar(g, t, e):
-            nc.scalar.activation(grouped(g, e, e + 1, t), xb[g][:, t, :].indirect(list_cols(e, e + 1)), COPY)
+        def gather_scalar(g, t, e, t_end):
+            window = xb[g][:, t:t_end, :].rearrange("p t n -> p (t n)")
+            nc.scalar.activation(grouped(g, e, e + 1, t), window.indirect(list_cols(e, e + 1)), COPY)
 
         def quantize(u0, u1):
             nc.vector.quantize_mx(
@@ -133,38 +134,41 @@ def tile_routed_moe_kernel(tc, xT, w, b, gate, offs, out):
 
         load_x(0, 0, 1)
         load_x(2, 0, 1)
+        nc.sync.dma_start(b_sb[:], b)
         load_x(0, 1, 2)
         load_x(2, 1, 2)
-        load_x(0, 2, 4)
-        load_x(2, 2, 4)
+        load_x(2, 2, 3)
+        load_x(0, 2, 3)
+        load_x(2, 3, 4)
+        load_x(0, 3, 4)
         load_x(1, 0, 2)
         load_x(3, 0, 2)
-        load_x(1, 2, 4)
         load_x(3, 2, 4)
+        load_x(1, 2, 4)
         load_w(0, 0)
-        load_w(1, 0)
         load_w(0, 1)
+        load_w(1, 0)
         load_w(1, 1)
         nc.sync.dma_start(gate_sb[:], gate)
-        nc.sync.dma_start(b_sb[:], b)
 
         cast(2, 0, 1)
         cast(2, 1, 2)
-        cast(2, 2, 4)
+        cast(2, 2, 3)
+        cast(2, 3, 4)
         cast(3, 0, 2)
-        cast(3, 2, 3)
-        cast(3, 3, 4)
+        cast(3, 2, 4)
         weights_interleave(0, 0)
-        weights_interleave(1, 0)
         weights_interleave(0, 1)
+        weights_interleave(1, 0)
         weights_interleave(1, 1)
 
         for t in range(PACK):
             for e in range(E):
-                gather_scalar(2, t, e)
-        for e in range(E):
-            for t in range(PACK):
-                gather_scalar(3, t, e)
+                gather_scalar(2, t, e, t + 1)
+        for t in range(PACK):
+            gather_scalar(3, t, 0, t + 1)
+        for t in range(PACK):
+            gather_scalar(3, t, 1, PACK)
 
         for t in range(PACK):
             gather_vector(0, t)
@@ -174,13 +178,15 @@ def tile_routed_moe_kernel(tc, xT, w, b, gate, offs, out):
         for t in (2, 3):
             gather_vector(1, t)
         quantize(2, 6)
-        quantize(6, 8)
-        for e in range(E):
-            for g in (0, 1):
-                multiply(e, g)
-        quantize(8, 10)
+        quantize(6, 7)
+        for g in (0, 1):
+            multiply(0, g)
+        quantize(7, 9)
         for g in (2, 3):
             multiply(0, g)
+        quantize(9, 10)
+        for g in (0, 1):
+            multiply(1, g)
         finish(0)
         quantize(10, 12)
         for g in (2, 3):

@@ -55,8 +55,8 @@ def tile_routed_moe_kernel(tc, xT, w, b, gate, offs, out):
         b_sb = keep.tile([P, E], F32, name="b_sb")
         gate_sb = keep.tile([P, E * C], F32, name="gate_sb")
 
-        token_piece = {(0, 0): 0, (0, 1): 1, (2, 0): 2, (2, 1): 3, (1, 0): 4, (1, 1): 5, (3, 0): 8, (3, 1): 11}
-        weight_piece = {(0, 0): 6, (0, 1): 7, (1, 0): 9, (1, 1): 10}
+        token_piece = {(0, 0): 0, (0, 1): 1, (2, 0): 2, (2, 1): 3, (1, 0): 4, (1, 1): 5, (3, 0): 6, (3, 1): 11}
+        weight_piece = {(0, 0): 7, (0, 1): 8, (1, 0): 9, (1, 1): 10}
         PIECES = 12
         row = keep.tile([P, PIECES * UNIT], BF16, name="row", align_bytes=64)
         codes = keep.tile([P, PIECES * C], U32, name="codes", align_bytes=64)
@@ -69,24 +69,28 @@ def tile_routed_moe_kernel(tc, xT, w, b, gate, offs, out):
             else:
                 nc.sync.dma_start(xs[g][:, t0:t1, :], x_view[g, :, t0:t1, :])
 
-        def load_w(e, h):
-            nc.sync.dma_start(w_raw[:, e, 2 * h : 2 * h + 2], w_view[e, :, 2 * h : 2 * h + 2])
+        def load_w(e, g0, g1):
+            nc.sync.dma_start(w_raw[:, e, g0:g1], w_view[e, :, g0:g1])
 
         def cast(g, t0, t1):
             nc.gpsimd.tensor_scalar(
                 out=xb[g][:, t0:t1, :], in0=xs[g][:, t0:t1, :], scalar1=1.0, scalar2=0.0, op0=MULT, op1=ADD
             )
 
-        def weights_interleave(e, h):
-            c0 = weight_piece[(e, h)] * UNIT
-            nc.gpsimd.tensor_scalar(
-                out=row[:, c0 : c0 + UNIT].rearrange("p (g n j) -> p g n j", g=2, j=PACK),
-                in0=w_raw[:, e, 2 * h : 2 * h + 2].rearrange("p g j n -> p g n j"),
-                scalar1=1.0,
-                scalar2=0.0,
-                op0=MULT,
-                op1=ADD,
+        def weight_views(e, g0, g1):
+            c0 = weight_piece[(e, g0 // 2)] * UNIT + (g0 % 2) * WUNIT
+            return (
+                row[:, c0 : c0 + (g1 - g0) * WUNIT].rearrange("p (g n j) -> p g n j", g=g1 - g0, j=PACK),
+                w_raw[:, e, g0:g1].rearrange("p g j n -> p g n j"),
             )
+
+        def weights_interleave(e, g0, g1):
+            grouped_w, raw_w = weight_views(e, g0, g1)
+            nc.gpsimd.tensor_scalar(out=grouped_w, in0=raw_w, scalar1=1.0, scalar2=0.0, op0=MULT, op1=ADD)
+
+        def weights_interleave_vector(e, g0, g1):
+            grouped_w, raw_w = weight_views(e, g0, g1)
+            nc.vector.tensor_copy(out=grouped_w, in_=raw_w)
 
         def grouped(g, e0, e1, t):
             c0 = token_piece[(g, e0)] * UNIT
@@ -134,7 +138,6 @@ def tile_routed_moe_kernel(tc, xT, w, b, gate, offs, out):
 
         load_x(0, 0, 1)
         load_x(2, 0, 1)
-        nc.sync.dma_start(b_sb[:], b)
         load_x(0, 1, 2)
         load_x(2, 1, 2)
         load_x(2, 2, 3)
@@ -145,10 +148,12 @@ def tile_routed_moe_kernel(tc, xT, w, b, gate, offs, out):
         load_x(3, 0, 2)
         load_x(3, 2, 4)
         load_x(1, 2, 4)
-        load_w(0, 0)
-        load_w(0, 1)
-        load_w(1, 0)
-        load_w(1, 1)
+        load_w(0, 0, 2)
+        load_w(0, 2, 4)
+        nc.sync.dma_start(b_sb[:], b)
+        load_w(1, 0, 2)
+        load_w(1, 2, 3)
+        load_w(1, 3, 4)
         nc.sync.dma_start(gate_sb[:], gate)
 
         cast(2, 0, 1)
@@ -157,10 +162,10 @@ def tile_routed_moe_kernel(tc, xT, w, b, gate, offs, out):
         cast(2, 3, 4)
         cast(3, 0, 2)
         cast(3, 2, 4)
-        weights_interleave(0, 0)
-        weights_interleave(0, 1)
-        weights_interleave(1, 0)
-        weights_interleave(1, 1)
+        weights_interleave(0, 0, 2)
+        weights_interleave(1, 0, 2)
+        weights_interleave(1, 2, 3)
+        weights_interleave(1, 3, 4)
 
         for t in range(PACK):
             for e in range(E):
@@ -178,10 +183,11 @@ def tile_routed_moe_kernel(tc, xT, w, b, gate, offs, out):
         for t in (2, 3):
             gather_vector(1, t)
         quantize(2, 6)
-        quantize(6, 7)
+        weights_interleave_vector(0, 2, 4)
+        quantize(6, 8)
         for g in (0, 1):
             multiply(0, g)
-        quantize(7, 9)
+        quantize(8, 9)
         for g in (2, 3):
             multiply(0, g)
         quantize(9, 10)

@@ -20,6 +20,7 @@ PACK = 4
 PASSES = K // (P * PACK)
 UNIT = C * PACK
 WUNIT = N * PACK
+SPLIT = 224
 
 
 def tile_routed_moe_kernel(tc, xT, w, b, gate, offs, out):
@@ -48,6 +49,7 @@ def tile_routed_moe_kernel(tc, xT, w, b, gate, offs, out):
         for g in (2, 3):
             xs[g] = keep.tile([P, PACK, T], F32, name="xs%d" % g)
             xb[g] = keep.tile([P, PACK, T], BF16, name="xb%d" % g)
+        xb1 = keep.tile([P, 2, T], BF16, name="xb1")
         w_raw = keep.tile([P, E, PASSES, PACK, N], F32, name="w_raw")
 
         acc = [psum.tile([P, 2 * C], F32, name="acc%d" % e) for e in range(E)]
@@ -76,6 +78,10 @@ def tile_routed_moe_kernel(tc, xT, w, b, gate, offs, out):
             nc.gpsimd.tensor_scalar(
                 out=xb[g][:, t0:t1, :], in0=xs[g][:, t0:t1, :], scalar1=1.0, scalar2=0.0, op0=MULT, op1=ADD
             )
+
+        def cast_pass_1():
+            q = place[(1, 2)]
+            nc.gpsimd.tensor_scalar(out=xb1[:], in0=xv[:, q : q + 2, :], scalar1=1.0, scalar2=0.0, op0=MULT, op1=ADD)
 
         def weight_views(e, g0, g1):
             c0 = weight_piece[(e, g0 // 2)] * UNIT + (g0 % 2) * WUNIT
@@ -108,6 +114,18 @@ def tile_routed_moe_kernel(tc, xT, w, b, gate, offs, out):
         def gather_scalar(g, t, e, t_end):
             window = xb[g][:, t:t_end, :].rearrange("p t n -> p (t n)")
             nc.scalar.activation(grouped(g, e, e + 1, t), window.indirect(list_cols(e, e + 1)), COPY)
+
+        def pass_1_slots(s0, s1, t):
+            c0 = token_piece[(1, 0)] * UNIT
+            return row[:, c0 + s0 * PACK : c0 + s1 * PACK].rearrange("p (n t) -> p n t", t=PACK)[:, :, t]
+
+        def gather_vector_pass_1(t):
+            nc.vector.tensor_copy(
+                pass_1_slots(SPLIT, T, t), xv[:, place[(1, t)], :].indirect(offsets[:, SPLIT // 16 : T // 16])
+            )
+
+        def gather_scalar_pass_1(t):
+            nc.scalar.activation(pass_1_slots(0, SPLIT, t), xb1[:, t - 2, :].indirect(offsets[:, 0 : SPLIT // 16]), COPY)
 
         def quantize(u0, u1):
             nc.vector.quantize_mx(
@@ -145,9 +163,9 @@ def tile_routed_moe_kernel(tc, xT, w, b, gate, offs, out):
         load_x(2, 3, 4)
         load_x(0, 3, 4)
         load_x(1, 0, 2)
+        load_x(1, 2, 4)
         load_x(3, 0, 2)
         load_x(3, 2, 4)
-        load_x(1, 2, 4)
         load_w(0, 0, 2)
         load_w(0, 2, 4)
         nc.sync.dma_start(b_sb[:], b)
@@ -160,6 +178,7 @@ def tile_routed_moe_kernel(tc, xT, w, b, gate, offs, out):
         cast(2, 1, 2)
         cast(2, 2, 3)
         cast(2, 3, 4)
+        cast_pass_1()
         cast(3, 0, 2)
         cast(3, 2, 4)
         weights_interleave(0, 0, 2)
@@ -170,6 +189,8 @@ def tile_routed_moe_kernel(tc, xT, w, b, gate, offs, out):
         for t in range(PACK):
             for e in range(E):
                 gather_scalar(2, t, e, t + 1)
+        for t in (2, 3):
+            gather_scalar_pass_1(t)
         for t in range(PACK):
             gather_scalar(3, t, 0, t + 1)
         for t in range(PACK):
@@ -181,7 +202,7 @@ def tile_routed_moe_kernel(tc, xT, w, b, gate, offs, out):
             gather_vector(1, t)
         quantize(0, 2)
         for t in (2, 3):
-            gather_vector(1, t)
+            gather_vector_pass_1(t)
         quantize(2, 6)
         weights_interleave_vector(0, 2, 4)
         quantize(6, 8)

@@ -12,6 +12,7 @@ U16 = mybir.dt.uint16
 U8 = mybir.dt.uint8
 FP8X4 = mybir.dt.float8_e4m3fn_x4
 COPY = mybir.ActivationFunctionType.Copy
+IDENTITY = mybir.ActivationFunctionType.Identity
 MULT = mybir.AluOpType.mult
 ADD = mybir.AluOpType.add
 
@@ -149,10 +150,8 @@ def tile_routed_moe_kernel(tc, xT, w, b, gate, offs, out):
 
         def finish(e):
             y = keep.tile([P, C], F32, name="y%d" % e)
-            nc.vector.scalar_tensor_tensor(
-                out=y[:], in0=acc[e][:, 0:C], scalar=b_sb[:, e : e + 1], in1=gate_sb[:, e * C : (e + 1) * C], op0=ADD, op1=MULT
-            )
-            nc.vector.tensor_copy(result[:].indirect(list_cols(e, e + 1)), y[:])
+            nc.scalar.activation(y[:], acc[e][:, 0:C], IDENTITY, bias=b_sb[:, e : e + 1])
+            nc.vector.tensor_tensor(result[:].indirect(list_cols(e, e + 1)), y[:], gate_sb[:, e * C : (e + 1) * C], MULT)
 
         load_x(0, 0, 1)
         load_x(2, 0, 1)

@@ -148,10 +148,15 @@ def tile_routed_moe_kernel(tc, xT, w, b, gate, offs, out):
                 stop=(g == PASSES - 1),
             )
 
-        def finish(e):
-            y = keep.tile([P, C], F32, name="y%d" % e)
-            nc.scalar.activation(y[:], acc[e][:, 0:C], IDENTITY, bias=b_sb[:, e : e + 1])
-            nc.vector.tensor_tensor(result[:].indirect(list_cols(e, e + 1)), y[:], gate_sb[:, e * C : (e + 1) * C], MULT)
+        y = {0: w_raw[:, 1, PASSES - 1].rearrange("p j n -> p (j n)")[:, 0:C]}
+        y1 = keep.tile([P, C], F32, name="y1")
+        y[1] = y1[:]
+
+        def read_sums(e):
+            nc.scalar.activation(y[e], acc[e][:, 0:C], IDENTITY, bias=b_sb[:, e : e + 1])
+
+        def scatter(e):
+            nc.vector.tensor_tensor(result[:].indirect(list_cols(e, e + 1)), y[e], gate_sb[:, e * C : (e + 1) * C], MULT)
 
         load_x(0, 0, 1)
         load_x(2, 0, 1)
@@ -213,10 +218,12 @@ def tile_routed_moe_kernel(tc, xT, w, b, gate, offs, out):
         quantize(9, 10)
         for g in (0, 1):
             multiply(1, g)
-        finish(0)
+        read_sums(0)
         quantize(10, 12)
         for g in (2, 3):
             multiply(1, g)
-        finish(1)
+        scatter(0)
+        read_sums(1)
+        scatter(1)
 
         nc.sync.dma_start(out, result[:])

@@ -21,7 +21,7 @@ PACK = 4
 PASSES = K // (P * PACK)
 UNIT = C * PACK
 WUNIT = N * PACK
-SPLIT = 224
+SPLIT = 320
 
 
 def tile_routed_moe_kernel(tc, xT, w, b, gate, offs, out):
@@ -187,8 +187,6 @@ def tile_routed_moe_kernel(tc, xT, w, b, gate, offs, out):
         cast(3, 2, 4)
         weights_interleave(0, 0, 2)
         weights_interleave(1, 0, 2)
-        weights_interleave(1, 2, 3)
-        weights_interleave(1, 3, 4)
 
         for t in range(PACK):
             for e in range(E):
@@ -218,6 +216,8 @@ def tile_routed_moe_kernel(tc, xT, w, b, gate, offs, out):
         quantize(9, 10)
         for g in (0, 1):
             multiply(1, g)
+        weights_interleave_vector(1, 2, 3)
+        weights_interleave_vector(1, 3, 4)
         read_sums(0)
         quantize(10, 12)
         for g in (2, 3):

@@ -96,8 +96,11 @@ def tile_routed_moe_kernel(tc, xT, w, b, gate, offs, out):
             nc.gpsimd.tensor_scalar(out=grouped_w, in0=raw_w, scalar1=1.0, scalar2=0.0, op0=MULT, op1=ADD)
 
         def weights_interleave_vector(e, g0, g1):
-            grouped_w, raw_w = weight_views(e, g0, g1)
-            nc.vector.tensor_copy(out=grouped_w, in_=raw_w)
+            c0 = weight_piece[(e, g0 // 2)] * UNIT + (g0 % 2) * WUNIT
+            nc.vector.tensor_copy(
+                out=row[:, c0 : c0 + (g1 - g0) * WUNIT].rearrange("p (g c i j) -> p g c j i", g=g1 - g0, i=PACK, j=PACK),
+                in_=w_raw[:, e, g0:g1].rearrange("p g j (c i) -> p g c j i", i=PACK),
+            )
 
         def grouped(g, e0, e1, t):
             c0 = token_piece[(g, e0)] * UNIT

@@ -175,10 +175,10 @@ def tile_routed_moe_kernel(tc, xT, w, b, gate, offs, out):
         load_x(3, 2, 4)
         load_w(0, 0, 2)
         load_w(0, 2, 4)
-        nc.sync.dma_start(b_sb[:], b)
         load_w(1, 0, 2)
         load_w(1, 2, 3)
         load_w(1, 3, 4)
+        nc.sync.dma_start(b_sb[:], b)
         nc.sync.dma_start(gate_sb[:], gate)
 
         cast(2, 0, 1)

@@ -44,13 +44,13 @@ def tile_routed_moe_kernel(tc, xT, w, b, gate, offs, out):
 
         xv = keep.tile([P, 2 * PACK + 1, T], F32, name="xv")
         nc.gpsimd.memset(xv[:, 2 * PACK, :], 0.0)
-        place = {(0, 0): 7, (0, 1): 6, (0, 2): 5, (0, 3): 4, (1, 0): 2, (1, 1): 3, (1, 2): 0, (1, 3): 1}
+        place = {(0, 0): 7, (0, 1): 6, (0, 2): 0, (0, 3): 1, (1, 0): 4, (1, 1): 5, (1, 2): 2, (1, 3): 3}
         xs = {}
         xb = {}
         for g in (2, 3):
             xs[g] = keep.tile([P, PACK, T], F32, name="xs%d" % g)
             xb[g] = keep.tile([P, PACK, T], BF16, name="xb%d" % g)
-        xb1 = keep.tile([P, 2, T], BF16, name="xb1")
+        xb0 = keep.tile([P, 2, T], BF16, name="xb0")
         w_raw = keep.tile([P, E, PASSES, PACK, N], F32, name="w_raw")
 
         acc = [psum.tile([P, 2 * C], F32, name="acc%d" % e) for e in range(E)]
@@ -80,9 +80,9 @@ def tile_routed_moe_kernel(tc, xT, w, b, gate, offs, out):
                 out=xb[g][:, t0:t1, :], in0=xs[g][:, t0:t1, :], scalar1=1.0, scalar2=0.0, op0=MULT, op1=ADD
             )
 
-        def cast_pass_1():
-            q = place[(1, 2)]
-            nc.gpsimd.tensor_scalar(out=xb1[:], in0=xv[:, q : q + 2, :], scalar1=1.0, scalar2=0.0, op0=MULT, op1=ADD)
+        def cast_pass_0():
+            q = place[(0, 2)]
+            nc.gpsimd.tensor_scalar(out=xb0[:], in0=xv[:, q : q + 2, :], scalar1=1.0, scalar2=0.0, op0=MULT, op1=ADD)
 
         def weight_views(e, g0, g1):
             c0 = weight_piece[(e, g0 // 2)] * UNIT + (g0 % 2) * WUNIT
@@ -119,17 +119,17 @@ def tile_routed_moe_kernel(tc, xT, w, b, gate, offs, out):
             window = xb[g][:, t:t_end, :].rearrange("p t n -> p (t n)")
             nc.scalar.activation(grouped(g, e, e + 1, t), window.indirect(list_cols(e, e + 1)), COPY)
 
-        def pass_1_slots(s0, s1, t):
-            c0 = token_piece[(1, 0)] * UNIT
+        def pass_0_slots(s0, s1, t):
+            c0 = token_piece[(0, 0)] * UNIT
             return row[:, c0 + s0 * PACK : c0 + s1 * PACK].rearrange("p (n t) -> p n t", t=PACK)[:, :, t]
 
-        def gather_vector_pass_1(t):
-            nc.vector.tensor_copy(
-                pass_1_slots(SPLIT, T, t), xv[:, place[(1, t)], :].indirect(offsets[:, SPLIT // 16 : T // 16])
-            )
+        def gather_vector_pass_0(t, planes):
+            q = place[(0, t)]
+            window = xv[:, q : q + planes, :].rearrange("p t n -> p (t n)")
+            nc.vector.tensor_copy(pass_0_slots(SPLIT, T, t), window.indirect(offsets[:, SPLIT // 16 : T // 16]))
 
-        def gather_scalar_pass_1(t):
-            nc.scalar.activation(pass_1_slots(0, SPLIT, t), xb1[:, t - 2, :].indirect(offsets[:, 0 : SPLIT // 16]), COPY)
+        def gather_scalar_pass_0(t):
+            nc.scalar.activation(pass_0_slots(0, SPLIT, t), xb0[:, t - 2, :].indirect(offsets[:, 0 : SPLIT // 16]), COPY)
 
         def quantize(u0, u1):
             nc.vector.quantize_mx(
@@ -166,10 +166,9 @@ def tile_routed_moe_kernel(tc, xT, w, b, gate, offs, out):
         load_x(0, 1, 2)
         load_x(2, 1, 2)
         load_x(2, 2, 3)
-        load_x(0, 2, 3)
-        load_x(2, 3, 4)
-        load_x(0, 3, 4)
         load_x(1, 0, 2)
+        load_x(2, 3, 4)
+        load_x(0, 2, 4)
         load_x(1, 2, 4)
         load_x(3, 0, 2)
         load_x(3, 2, 4)
@@ -185,7 +184,7 @@ def tile_routed_moe_kernel(tc, xT, w, b, gate, offs, out):
         cast(2, 1, 2)
         cast(2, 2, 3)
         cast(2, 3, 4)
-        cast_pass_1()
+        cast_pass_0()
         cast(3, 0, 2)
         cast(3, 2, 4)
         weights_interleave(0, 0, 2)
@@ -195,20 +194,20 @@ def tile_routed_moe_kernel(tc, xT, w, b, gate, offs, out):
             for e in range(E):
                 gather_scalar(2, t, e, t + 1)
         for t in (2, 3):
-            gather_scalar_pass_1(t)
+            gather_scalar_pass_0(t)
         for t in range(PACK):
             gather_scalar(3, t, 0, t + 1)
         for t in range(PACK):
             gather_scalar(3, t, 1, PACK)
 
-        for t in range(PACK):
-            gather_vector(0, t)
         for t in (0, 1):
+            gather_vector(0, t)
+        for t in range(PACK):
             gather_vector(1, t)
-        quantize(0, 2)
-        for t in (2, 3):
-            gather_vector_pass_1(t)
+        gather_vector_pass_0(2, 1)
+        gather_vector_pass_0(3, 2)
         quantize(2, 6)
+        quantize(0, 2)
         weights_interleave_vector(0, 2, 4)
         quantize(6, 8)
         for g in (0, 1):

@@ -161,17 +161,17 @@ def tile_routed_moe_kernel(tc, xT, w, b, gate, offs, out):
         def scatter(e):
             nc.vector.tensor_tensor(result[:].indirect(list_cols(e, e + 1)), y[e], gate_sb[:, e * C : (e + 1) * C], MULT)
 
-        load_x(0, 0, 1)
         load_x(2, 0, 1)
-        load_x(0, 1, 2)
+        load_x(0, 0, 1)
         load_x(2, 1, 2)
+        load_x(0, 1, 2)
         load_x(2, 2, 3)
         load_x(1, 0, 2)
         load_x(2, 3, 4)
         load_x(0, 2, 4)
         load_x(1, 2, 4)
-        load_x(3, 0, 2)
-        load_x(3, 2, 4)
+        for t in range(PACK):
+            load_x(3, t, t + 1)
         load_w(0, 0, 2)
         load_w(0, 2, 4)
         load_w(1, 0, 2)
@@ -185,8 +185,8 @@ def tile_routed_moe_kernel(tc, xT, w, b, gate, offs, out):
         cast(2, 2, 3)
         cast(2, 3, 4)
         cast_pass_0()
-        cast(3, 0, 2)
-        cast(3, 2, 4)
+        for t in range(PACK):
+            cast(3, t, t + 1)
         weights_interleave(0, 0, 2)
         weights_interleave(1, 0, 2)
 
@@ -215,12 +215,12 @@ def tile_routed_moe_kernel(tc, xT, w, b, gate, offs, out):
         quantize(8, 9)
         for g in (2, 3):
             multiply(0, g)
-        quantize(9, 10)
-        for g in (0, 1):
-            multiply(1, g)
         weights_interleave_vector(1, 2, 3)
         weights_interleave_vector(1, 3, 4)
         read_sums(0)
+        quantize(9, 10)
+        for g in (0, 1):
+            multiply(1, g)
         quantize(10, 12)
         for g in (2, 3):
             multiply(1, g)

@@ -61,7 +61,9 @@ def tile_routed_moe_kernel(tc, xT, w, b, gate, offs, out):
         token_piece = {(0, 0): 0, (0, 1): 1, (2, 0): 2, (2, 1): 3, (1, 0): 4, (1, 1): 5, (3, 0): 6, (3, 1): 11}
         weight_piece = {(0, 0): 7, (0, 1): 8, (1, 0): 9, (1, 1): 10}
         PIECES = 12
-        row = keep.tile([P, PIECES * UNIT], BF16, name="row", align_bytes=64)
+        row_place = {0: 0, 1: 1, 2: 2, 3: 3, 4: 4, 5: 5, 6: 6, 7: 7, 8: 9, 9: 10, 10: 7, 11: 8}
+        ROW_PLACES = 11
+        row = keep.tile([P, ROW_PLACES * UNIT], BF16, name="row", align_bytes=64)
         codes = keep.tile([P, PIECES * C], U32, name="codes", align_bytes=64)
         scales = keep.tile([P, PIECES * C], U8, name="scales", align_bytes=64)
 
@@ -85,7 +87,7 @@ def tile_routed_moe_kernel(tc, xT, w, b, gate, offs, out):
             nc.gpsimd.tensor_scalar(out=xb0[:], in0=xv[:, q : q + 2, :], scalar1=1.0, scalar2=0.0, op0=MULT, op1=ADD)
 
         def weight_views(e, g0, g1):
-            c0 = weight_piece[(e, g0 // 2)] * UNIT + (g0 % 2) * WUNIT
+            c0 = row_place[weight_piece[(e, g0 // 2)]] * UNIT + (g0 % 2) * WUNIT
             return (
                 row[:, c0 : c0 + (g1 - g0) * WUNIT].rearrange("p (g n j) -> p g n j", g=g1 - g0, j=PACK),
                 w_raw[:, e, g0:g1].rearrange("p g j n -> p g n j"),
@@ -96,14 +98,14 @@ def tile_routed_moe_kernel(tc, xT, w, b, gate, offs, out):
             nc.gpsimd.tensor_scalar(out=grouped_w, in0=raw_w, scalar1=1.0, scalar2=0.0, op0=MULT, op1=ADD)
 
         def weights_interleave_vector(e, g0, g1):
-            c0 = weight_piece[(e, g0 // 2)] * UNIT + (g0 % 2) * WUNIT
+            c0 = row_place[weight_piece[(e, g0 // 2)]] * UNIT + (g0 % 2) * WUNIT
             nc.vector.tensor_copy(
                 out=row[:, c0 : c0 + (g1 - g0) * WUNIT].rearrange("p (g c i j) -> p g c j i", g=g1 - g0, i=PACK, j=PACK),
                 in_=w_raw[:, e, g0:g1].rearrange("p g j (c i) -> p g c j i", i=PACK),
             )
 
         def grouped(g, e0, e1, t):
-            c0 = token_piece[(g, e0)] * UNIT
+            c0 = row_place[token_piece[(g, e0)]] * UNIT
             c1 = c0 + (e1 - e0) * UNIT
             return row[:, c0:c1].rearrange("p (n t) -> p n t", t=PACK)[:, :, t]
 
@@ -135,7 +137,7 @@ def tile_routed_moe_kernel(tc, xT, w, b, gate, offs, out):
             nc.vector.quantize_mx(
                 out=codes[:, u0 * C : u1 * C].bitcast(FP8X4),
                 scales=scales[:, u0 * C : u1 * C],
-                in_=row[:, u0 * UNIT : u1 * UNIT],
+                in_=row[:, row_place[u0] * UNIT : (row_place[u0] + u1 - u0) * UNIT],
             )
 
         def multiply(e, g):

@@ -44,7 +44,7 @@ def tile_routed_moe_kernel(tc, xT, w, b, gate, offs, out):
 
         xv = keep.tile([P, 2 * PACK + 1, T], F32, name="xv")
         nc.gpsimd.memset(xv[:, 2 * PACK, :], 0.0)
-        place = {(0, 0): 7, (0, 1): 6, (0, 2): 0, (0, 3): 1, (1, 0): 4, (1, 1): 5, (1, 2): 2, (1, 3): 3}
+        place = {(0, 0): 7, (0, 1): 6, (0, 2): 2, (0, 3): 3, (1, 0): 4, (1, 1): 5, (1, 2): 0, (1, 3): 1}
         xs = {}
         xb = {}
         for g in (2, 3):
@@ -168,10 +168,12 @@ def tile_routed_moe_kernel(tc, xT, w, b, gate, offs, out):
         load_x(2, 1, 2)
         load_x(0, 1, 2)
         load_x(2, 2, 3)
-        load_x(1, 0, 2)
+        load_x(1, 1, 2)
+        load_x(1, 0, 1)
         load_x(2, 3, 4)
         load_x(0, 2, 4)
-        load_x(1, 2, 4)
+        load_x(1, 3, 4)
+        load_x(1, 2, 3)
         for t in range(PACK):
             load_x(3, t, t + 1)
         load_w(0, 0, 2)
@@ -204,10 +206,12 @@ def tile_routed_moe_kernel(tc, xT, w, b, gate, offs, out):
 
         for t in (0, 1):
             gather_vector(0, t)
-        for t in range(PACK):
+        for t in (1, 0):
             gather_vector(1, t)
         gather_vector_pass_0(2, 1)
-        gather_vector_pass_0(3, 2)
+        gather_vector_pass_0(3, 1)
+        for t in (3, 2):
+            gather_vector(1, t)
         quantize(2, 6)
         quantize(0, 2)
         weights_interleave_vector(0, 2, 4)

@@ -21,7 +21,7 @@ PACK = 4
 PASSES = K // (P * PACK)
 UNIT = C * PACK
 WUNIT = N * PACK
-SPLIT = 320
+SPLIT = 384
 
 
 def tile_routed_moe_kernel(tc, xT, w, b, gate, offs, out):

@@ -192,7 +192,6 @@ def tile_routed_moe_kernel(tc, xT, w, b, gate, offs, out):
         for t in range(PACK):
             cast(3, t, t + 1)
         weights_interleave(0, 0, 2)
-        weights_interleave(1, 0, 2)
 
         for t in range(PACK):
             for e in range(E):
@@ -221,6 +220,7 @@ def tile_routed_moe_kernel(tc, xT, w, b, gate, offs, out):
         quantize(8, 9)
         for g in (2, 3):
             multiply(0, g)
+        weights_interleave_vector(1, 0, 2)
         weights_interleave_vector(1, 2, 3)
         weights_interleave_vector(1, 3, 4)
         read_sums(0)

@@ -32,7 +32,6 @@ def tile_routed_moe_kernel(tc, xT, w, b, gate, offs, out):
         psum = ctx.enter_context(tc.psum_pool(name="psum", bufs=1))
 
         offsets = lists.tile([P, E * C // 16], U16, name="offsets")
-        nc.sync.dma_start(offsets[:], offs)
 
         warm_in = keep.tile([P, 1], F32, name="warm_in")
         warm_out = keep.tile([P, 1], F32, name="warm_out")
@@ -44,7 +43,7 @@ def tile_routed_moe_kernel(tc, xT, w, b, gate, offs, out):
 
         xv = keep.tile([P, 2 * PACK + 1, T], F32, name="xv")
         nc.gpsimd.memset(xv[:, 2 * PACK, :], 0.0)
-        place = {(0, 0): 7, (0, 1): 6, (0, 2): 2, (0, 3): 3, (1, 0): 4, (1, 1): 5, (1, 2): 0, (1, 3): 1}
+        place = {(1, 0): 7, (1, 1): 6, (1, 2): 5, (1, 3): 4, (0, 2): 2, (0, 3): 3, (0, 1): 1, (0, 0): 0}
         xs = {}
         xb = {}
         for g in (2, 3):
@@ -164,16 +163,17 @@ def tile_routed_moe_kernel(tc, xT, w, b, gate, offs, out):
             nc.vector.tensor_tensor(result[:].indirect(list_cols(e, e + 1)), y[e], gate_sb[:, e * C : (e + 1) * C], MULT)
 
         load_x(2, 0, 1)
-        load_x(0, 0, 1)
-        load_x(2, 1, 2)
-        load_x(0, 1, 2)
-        load_x(2, 2, 3)
-        load_x(1, 1, 2)
+        nc.sync.dma_start(offsets[:], offs)
         load_x(1, 0, 1)
+        load_x(2, 1, 2)
+        load_x(1, 1, 2)
+        load_x(2, 2, 3)
+        load_x(1, 2, 3)
+        load_x(1, 3, 4)
         load_x(2, 3, 4)
         load_x(0, 2, 4)
-        load_x(1, 3, 4)
-        load_x(1, 2, 3)
+        load_x(0, 1, 2)
+        load_x(0, 0, 1)
         for t in range(PACK):
             load_x(3, t, t + 1)
         load_w(0, 0, 2)
@@ -184,7 +184,7 @@ def tile_routed_moe_kernel(tc, xT, w, b, gate, offs, out):
         nc.sync.dma_start(b_sb[:], b)
         nc.sync.dma_start(gate_sb[:], gate)
 
-        cast(2, 0, 1)
+        nc.vector.tensor_copy(out=xb[2][:, 0:1, :], in_=xs[2][:, 0:1, :])
         cast(2, 1, 2)
         cast(2, 2, 3)
         cast(2, 3, 4)
@@ -203,14 +203,12 @@ def tile_routed_moe_kernel(tc, xT, w, b, gate, offs, out):
         for t in range(PACK):
             gather_scalar(3, t, 1, PACK)
 
-        for t in (0, 1):
-            gather_vector(0, t)
-        for t in (1, 0):
+        for t in range(PACK):
             gather_vector(1, t)
         gather_vector_pass_0(2, 1)
         gather_vector_pass_0(3, 1)
-        for t in (3, 2):
-            gather_vector(1, t)
+        for t in (1, 0):
+            gather_vector(0, t)
         quantize(2, 6)
         quantize(0, 2)
         weights_interleave_vector(0, 2, 4)

@@ -43,7 +43,7 @@ def tile_routed_moe_kernel(tc, xT, w, b, gate, offs, out):
 
         xv = keep.tile([P, 2 * PACK + 1, T], F32, name="xv")
         nc.gpsimd.memset(xv[:, 2 * PACK, :], 0.0)
-        place = {(1, 0): 7, (1, 1): 6, (1, 2): 5, (1, 3): 4, (0, 2): 2, (0, 3): 3, (0, 1): 1, (0, 0): 0}
+        place = {(0, 0): 7, (0, 1): 6, (0, 2): 2, (0, 3): 3, (1, 0): 4, (1, 1): 5, (1, 2): 0, (1, 3): 1}
         xs = {}
         xb = {}
         for g in (2, 3):
@@ -164,16 +164,16 @@ def tile_routed_moe_kernel(tc, xT, w, b, gate, offs, out):
 
         load_x(2, 0, 1)
         nc.sync.dma_start(offsets[:], offs)
-        load_x(1, 0, 1)
+        load_x(0, 0, 1)
         load_x(2, 1, 2)
-        load_x(1, 1, 2)
+        load_x(0, 1, 2)
         load_x(2, 2, 3)
-        load_x(1, 2, 3)
-        load_x(1, 3, 4)
+        load_x(1, 1, 2)
+        load_x(1, 0, 1)
         load_x(2, 3, 4)
         load_x(0, 2, 4)
-        load_x(0, 1, 2)
-        load_x(0, 0, 1)
+        load_x(1, 3, 4)
+        load_x(1, 2, 3)
         for t in range(PACK):
             load_x(3, t, t + 1)
         load_w(0, 0, 2)
@@ -203,12 +203,14 @@ def tile_routed_moe_kernel(tc, xT, w, b, gate, offs, out):
         for t in range(PACK):
             gather_scalar(3, t, 1, PACK)
 
-        for t in range(PACK):
+        for t in (0, 1):
+            gather_vector(0, t)
+        for t in (1, 0):
             gather_vector(1, t)
         gather_vector_pass_0(2, 1)
         gather_vector_pass_0(3, 1)
-        for t in (1, 0):
-            gather_vector(0, t)
+        for t in (3, 2):
+            gather_vector(1, t)
         quantize(2, 6)
         quantize(0, 2)
         weights_interleave_vector(0, 2, 4)

from contextlib import ExitStack

import concourse.mybir as mybir

K, T, E, C, N = 2048, 512, 2, 256, 128
FLOPS = 2 * K * N * E * C

F32 = mybir.dt.float32
BF16 = mybir.dt.bfloat16
U32 = mybir.dt.uint32
U16 = mybir.dt.uint16
U8 = mybir.dt.uint8
FP8X4 = mybir.dt.float8_e4m3fn_x4
COPY = mybir.ActivationFunctionType.Copy
IDENTITY = mybir.ActivationFunctionType.Identity
MULT = mybir.AluOpType.mult
ADD = mybir.AluOpType.add

P = 128
PACK = 4
PASSES = K // (P * PACK)
UNIT = C * PACK
WUNIT = N * PACK
SPLIT = 384


def tile_routed_moe_kernel(tc, xT, w, b, gate, offs, out):
    nc = tc.nc
    with ExitStack() as ctx:
        lists = ctx.enter_context(tc.tile_pool(name="lists", bufs=1))
        keep = ctx.enter_context(tc.tile_pool(name="keep", bufs=1))
        psum = ctx.enter_context(tc.psum_pool(name="psum", bufs=1))

        offsets = lists.tile([P, E * C // 16], U16, name="offsets")

        warm_in = keep.tile([P, 1], F32, name="warm_in")
        warm_out = keep.tile([P, 1], F32, name="warm_out")
        nc.gpsimd.memset(warm_in[:], 0.0)
        nc.scalar.activation(warm_out[:], warm_in[:], COPY)

        x_view = xT.rearrange("(g p t) n -> g p t n", p=P, t=PACK)
        w_view = w.rearrange("e (g p j) n -> e p g j n", p=P, j=PACK)

        xv = keep.tile([P, 2 * PACK + 1, T], F32, name="xv")
        nc.gpsimd.memset(xv[:, 2 * PACK, :], 0.0)
        place = {(0, 0): 7, (0, 1): 6, (0, 2): 2, (0, 3): 3, (1, 0): 4, (1, 1): 5, (1, 2): 0, (1, 3): 1}
        xs = {}
        xb = {}
        for g in (2, 3):
            xs[g] = keep.tile([P, PACK, T], F32, name="xs%d" % g)
            xb[g] = keep.tile([P, PACK, T], BF16, name="xb%d" % g)
        xb0 = keep.tile([P, 2, T], BF16, name="xb0")
        w_raw = keep.tile([P, E, PASSES, PACK, N], F32, name="w_raw")

        acc = [psum.tile([P, 2 * C], F32, name="acc%d" % e) for e in range(E)]
        result = keep.tile([P, T], F32, name="result")
        b_sb = keep.tile([P, E], F32, name="b_sb")
        gate_sb = keep.tile([P, E * C], F32, name="gate_sb")

        token_piece = {(0, 0): 0, (0, 1): 1, (2, 0): 2, (2, 1): 3, (1, 0): 4, (1, 1): 5, (3, 0): 6, (3, 1): 11}
        weight_piece = {(0, 0): 7, (0, 1): 8, (1, 0): 9, (1, 1): 10}
        PIECES = 12
        row_place = {0: 0, 1: 1, 2: 2, 3: 3, 4: 4, 5: 5, 6: 6, 7: 7, 8: 9, 9: 10, 10: 7, 11: 8}
        ROW_PLACES = 11
        row = keep.tile([P, ROW_PLACES * UNIT], BF16, name="row", align_bytes=64)
        codes = keep.tile([P, PIECES * C], U32, name="codes", align_bytes=64)
        scales = keep.tile([P, PIECES * C], U8, name="scales", align_bytes=64)

        def load_x(g, t0, t1):
            if g < 2:
                q = place[(g, t0)]
                nc.sync.dma_start(xv[:, q : q + t1 - t0, :], x_view[g, :, t0:t1, :])
            else:
                nc.sync.dma_start(xs[g][:, t0:t1, :], x_view[g, :, t0:t1, :])

        def load_w(e, g0, g1):
            nc.sync.dma_start(w_raw[:, e, g0:g1], w_view[e, :, g0:g1])

        def cast(g, t0, t1):
            nc.gpsimd.tensor_scalar(
                out=xb[g][:, t0:t1, :], in0=xs[g][:, t0:t1, :], scalar1=1.0, scalar2=0.0, op0=MULT, op1=ADD
            )

        def cast_pass_0():
            q = place[(0, 2)]
            nc.gpsimd.tensor_scalar(out=xb0[:], in0=xv[:, q : q + 2, :], scalar1=1.0, scalar2=0.0, op0=MULT, op1=ADD)

        def weight_views(e, g0, g1):
            c0 = row_place[weight_piece[(e, g0 // 2)]] * UNIT + (g0 % 2) * WUNIT
            return (
                row[:, c0 : c0 + (g1 - g0) * WUNIT].rearrange("p (g n j) -> p g n j", g=g1 - g0, j=PACK),
                w_raw[:, e, g0:g1].rearrange("p g j n -> p g n j"),
            )

        def weights_interleave(e, g0, g1):
            grouped_w, raw_w = weight_views(e, g0, g1)
            nc.gpsimd.tensor_scalar(out=grouped_w, in0=raw_w, scalar1=1.0, scalar2=0.0, op0=MULT, op1=ADD)

        def weights_interleave_vector(e, g0, g1):
            c0 = row_place[weight_piece[(e, g0 // 2)]] * UNIT + (g0 % 2) * WUNIT
            nc.vector.tensor_copy(
                out=row[:, c0 : c0 + (g1 - g0) * WUNIT].rearrange("p (g c i j) -> p g c j i", g=g1 - g0, i=PACK, j=PACK),
                in_=w_raw[:, e, g0:g1].rearrange("p g j (c i) -> p g c j i", i=PACK),
            )

        def grouped(g, e0, e1, t):
            c0 = row_place[token_piece[(g, e0)]] * UNIT
            c1 = c0 + (e1 - e0) * UNIT
            return row[:, c0:c1].rearrange("p (n t) -> p n t", t=PACK)[:, :, t]

        def list_cols(e0, e1):
            return offsets[:, e0 * C // 16 : e1 * C // 16]

        def gather_vector(g, t):
            q = place[(g, t)]
            window = xv[:, q : q + 2, :].rearrange("p t n -> p (t n)")
            nc.vector.tensor_copy(grouped(g, 0, E, t), window.indirect(list_cols(0, E)))

        def gather_scalar(g, t, e, t_end):
            window = xb[g][:, t:t_end, :].rearrange("p t n -> p (t n)")
            nc.scalar.activation(grouped(g, e, e + 1, t), window.indirect(list_cols(e, e + 1)), COPY)

        def pass_0_slots(s0, s1, t):
            c0 = token_piece[(0, 0)] * UNIT
            return row[:, c0 + s0 * PACK : c0 + s1 * PACK].rearrange("p (n t) -> p n t", t=PACK)[:, :, t]

        def gather_vector_pass_0(t, planes):
            q = place[(0, t)]
            window = xv[:, q : q + planes, :].rearrange("p t n -> p (t n)")
            nc.vector.tensor_copy(pass_0_slots(SPLIT, T, t), window.indirect(offsets[:, SPLIT // 16 : T // 16]))

        def gather_scalar_pass_0(t):
            nc.scalar.activation(pass_0_slots(0, SPLIT, t), xb0[:, t - 2, :].indirect(offsets[:, 0 : SPLIT // 16]), COPY)

        def quantize(u0, u1):
            nc.vector.quantize_mx(
                out=codes[:, u0 * C : u1 * C].bitcast(FP8X4),
                scales=scales[:, u0 * C : u1 * C],
                in_=row[:, row_place[u0] * UNIT : (row_place[u0] + u1 - u0) * UNIT],
            )

        def multiply(e, g):
            c0 = token_piece[(g, e)] * C
            w0 = weight_piece[(e, g // 2)] * C + (g % 2) * N
            nc.tensor.matmul_mx(
                out=acc[e][:, 0:C],
                lhsT=codes[:, w0 : w0 + N].bitcast(FP8X4),
                lhsT_scale=scales[:, w0 : w0 + N],
                rhs=codes[:, c0 : c0 + C].bitcast(FP8X4),
                rhs_scale=scales[:, c0 : c0 + C],
                start=(g == 0),
                stop=(g == PASSES - 1),
            )

        y = {0: w_raw[:, 1, PASSES - 1].rearrange("p j n -> p (j n)")[:, 0:C]}
        y1 = keep.tile([P, C], F32, name="y1")
        y[1] = y1[:]

        def read_sums(e):
            nc.scalar.activation(y[e], acc[e][:, 0:C], IDENTITY, bias=b_sb[:, e : e + 1])

        def scatter(e):
            nc.vector.tensor_tensor(result[:].indirect(list_cols(e, e + 1)), y[e], gate_sb[:, e * C : (e + 1) * C], MULT)

        load_x(2, 0, 1)
        nc.sync.dma_start(offsets[:], offs)
        load_x(0, 0, 1)
        load_x(2, 1, 2)
        load_x(0, 1, 2)
        load_x(2, 2, 3)
        load_x(1, 1, 2)
        load_x(1, 0, 1)
        load_x(2, 3, 4)
        load_x(0, 2, 4)
        load_x(1, 3, 4)
        load_x(1, 2, 3)
        for t in range(PACK):
            load_x(3, t, t + 1)
        load_w(0, 0, 2)
        load_w(0, 2, 4)
        load_w(1, 0, 2)
        load_w(1, 2, 3)
        load_w(1, 3, 4)
        nc.sync.dma_start(b_sb[:], b)
        nc.sync.dma_start(gate_sb[:], gate)

        nc.vector.tensor_copy(out=xb[2][:, 0:1, :], in_=xs[2][:, 0:1, :])
        cast(2, 1, 2)
        cast(2, 2, 3)
        cast(2, 3, 4)
        cast_pass_0()
        for t in range(PACK):
            cast(3, t, t + 1)
        weights_interleave(0, 0, 2)

        for t in range(PACK):
            for e in range(E):
                gather_scalar(2, t, e, t + 1)
        for t in (2, 3):
            gather_scalar_pass_0(t)
        for t in range(PACK):
            gather_scalar(3, t, 0, t + 1)
        for t in range(PACK):
            gather_scalar(3, t, 1, PACK)

        for t in (0, 1):
            gather_vector(0, t)
        for t in (1, 0):
            gather_vector(1, t)
        gather_vector_pass_0(2, 1)
        gather_vector_pass_0(3, 1)
        for t in (3, 2):
            gather_vector(1, t)
        quantize(2, 6)
        quantize(0, 2)
        weights_interleave_vector(0, 2, 4)
        quantize(6, 8)
        for g in (0, 1):
            multiply(0, g)
        quantize(8, 9)
        for g in (2, 3):
            multiply(0, g)
        weights_interleave_vector(1, 0, 2)
        weights_interleave_vector(1, 2, 3)
        weights_interleave_vector(1, 3, 4)
        read_sums(0)
        quantize(9, 10)
        for g in (0, 1):
            multiply(1, g)
        quantize(10, 12)
        for g in (2, 3):
            multiply(1, g)
        scatter(0)
        read_sums(1)
        scatter(1)

        nc.sync.dma_start(out, result[:])
